import numpy as np
import ml_dtypes


def mxq(x, axis, fmt="e4m3"):
    dtype, down = {"e4m3": (ml_dtypes.float8_e4m3fn, 7), "e5m2": (ml_dtypes.float8_e5m2, 14)}[fmt]
    v = np.moveaxis(np.asarray(x, np.float32).astype(ml_dtypes.bfloat16).astype(np.float64), axis, -1)
    blocks = v.reshape(v.shape[:-1] + (-1, 32))
    amax = np.abs(blocks).max(-1, keepdims=True)
    byte = np.maximum(np.where(amax > 0, np.frexp(amax)[1] - 1 + 127, 0) - down, 1)
    scale = np.exp2(byte - 127.0)
    codes = (blocks / scale).astype(np.float32).astype(dtype).astype(np.float64)
    return np.moveaxis((codes * scale).reshape(v.shape), -1, axis)


WIDE = False


def mx_kscale(k):
    if not WIDE:
        return np.ones(k)
    levels = np.array([10, -10, 5, -5, 0])
    if k % 512:
        return np.exp2(np.random.permutation(np.resize(levels, k // 32))).repeat(32)
    a = np.empty((k // 512, 16))
    for p in range(k // 512):
        a[p, :8] = np.random.permutation(np.resize(levels, 8))
        for g in range(8):
            far = levels[np.abs(levels - a[p, g]) >= 10]
            a[p, g + 8] = far[np.random.randint(len(far))]
    return np.exp2(a.ravel()).repeat(32)


def f64(x):
    return np.asarray(x).astype(np.float64)


def striped(idx):
    return np.tile(idx.reshape(-1, 16).T, (8, 1)).astype(np.uint16)


def unstriped(offs):
    return offs[:16].T.reshape(-1).astype(np.int64)


def striped8(idx):
    return np.concatenate([x.reshape(-1, 16).T for x in idx]).astype(np.uint16)


def runs(offs, k):
    lists = np.stack([offs[16 * r : 16 * r + 16].T.reshape(-1) for r in range(8)]).astype(np.int64)
    return lists[np.arange(k) % 512 // 64]


def pack_weight(w):
    k, n = w.shape
    w = f64(np.asarray(w, np.float32).astype(ml_dtypes.bfloat16)).reshape(k // 32, 32, n)
    amax = np.abs(w).max(1)
    byte = np.clip(np.where(amax > 0, np.frexp(amax)[1] - 1 + 127 - 7, 1), 1, 254)
    scaled = (w * np.exp2(127.0 - byte)[:, None, :]).reshape(k, n).astype(np.float32)
    words = np.ascontiguousarray(scaled.reshape(k // 512, 128, 4, n).transpose(0, 1, 3, 2)).astype(ml_dtypes.float8_e4m3fn).view(np.uint8)
    return words, np.ascontiguousarray(byte.astype(np.uint8).reshape(k // 512, 16, n))


def unpack_weight(words, scales):
    g, p, n, _ = words.shape
    vals = np.ascontiguousarray(words).view(ml_dtypes.float8_e4m3fn).astype(np.float64) * np.repeat(np.exp2(scales.astype(np.float64) - 127.0), 8, axis=1)[..., None]
    return vals.transpose(0, 1, 3, 2).reshape(g * 512, n)

def planes(y):
    n, m = y.shape
    v = y.astype(np.float32).astype(ml_dtypes.bfloat16).astype(np.float64).reshape(n // 32, 32, m)
    top = np.abs(v).max(1)
    byte = np.clip(np.where(top > 0, np.frexp(top)[1] - 1 + 127 - 7, 1), 1, 254)
    codes = (v * np.exp2(127.0 - byte)[:, None, :]).reshape(n, m).astype(np.float32).astype(ml_dtypes.float8_e4m3fn).view(np.uint8)
    words = codes.reshape(n // 512, 128, 4, m).transpose(0, 1, 3, 2)
    return np.ascontiguousarray(words), np.ascontiguousarray(byte.astype(np.uint8).reshape(n // 512, 16, m))


K, T, S, N, H, U = 512, 2048, 512, 512, 512, 1024


def setup_inputs():
    n = np.random.standard_normal
    s = mx_kscale(K)[:, None]
    u = mx_kscale(H)
    packed_xT = pack_weight(n((K, T)) * s)
    packed_w1 = pack_weight(n((K, H)) / np.sqrt(K) / s)
    packed_w2 = pack_weight(n((H, N)) / np.sqrt(H) / u[:, None])
    return {
        "x_words": packed_xT[0],
        "x_scales": packed_xT[1],
        "w1_words": packed_w1[0],
        "w1_scales": packed_w1[1],
        "ef": n((H, U)).astype(np.float32),
        "gn": (np.random.uniform(0.5, 1.5, (H, 1)) * u[:, None]).astype(np.float32),
        "w2_words": packed_w2[0],
        "w2_scales": packed_w2[1],
        "offs": striped(np.random.permutation(T)[:S]),
        "ent": striped8(np.stack([np.random.permutation(U)[:S] for _ in range(8)])),
    }


def reference(x_words, x_scales, w1_words, w1_scales, ef, gn, w2_words, w2_scales, offs, ent):
    xq = unpack_weight(x_words, x_scales)[:, unstriped(offs)]
    y = unpack_weight(w1_words, w1_scales).T @ xq
    a = y + f64(ef)[np.arange(H)[:, None], runs(ent, H)]
    sent = np.clip(a, -0.5, 0.5)
    z = f64(gn) * (sent + 0.25 * (a - sent))
    out_0 = unpack_weight(w2_words, w2_scales).T @ mxq(z, 0, "e4m3")
    return (out_0,) + planes(out_0)

@@ -1,0 +1,224 @@
+from contextlib import ExitStack
+
+import concourse.mybir as mybir
+
+K, T, S, N, H, U = 512, 2048, 512, 512, 512, 1024
+FLOPS = 2 * K * H * S + 2 * H * N * S
+
+F32 = mybir.dt.float32
+BF16 = mybir.dt.bfloat16
+I32 = mybir.dt.int32
+U32 = mybir.dt.uint32
+U16 = mybir.dt.uint16
+U8 = mybir.dt.uint8
+FP8X4 = mybir.dt.float8_e4m3fn_x4
+ALU = mybir.AluOpType
+ACT = mybir.ActivationFunctionType
+
+P = 128
+PACK = 4
+HALF = 256
+CHUNK = 128
+W1_ROW = 4
+W2_ROW = 8
+
+
+def tile_picked_errfb_none_po_kernel(
+    tc, x_words, x_scales, w1_words, w1_scales, ef, gn, w2_words, w2_scales, offs, ent, out_0, out_1, out_2
+):
+    nc = tc.nc
+    with ExitStack() as ctx:
+        sb = ctx.enter_context(tc.tile_pool(name="sb", bufs=1))
+        shared = ctx.enter_context(tc.tile_pool(name="shared", bufs=1))
+        ps = ctx.enter_context(tc.psum_pool(name="ps", bufs=1))
+
+        def tile(shape, dtype, name):
+            return sb.tile(shape, dtype, name=name, align_bytes=64)
+
+        def placed(shape, dtype, name, offset):
+            return shared.tile(shape, dtype, name=name, align_bytes=64, offset=offset)
+
+        def words(dram):
+            return dram[0].rearrange("p n t -> p (n t)").bitcast(I32)
+
+        def load_scale_rows(queue, plane, first, dram):
+            for q in range(4):
+                queue.dma_start(
+                    out=plane[32 * q + first : 32 * q + first + 4, :].bitcast(I32),
+                    in_=dram[0, 4 * q : 4 * q + 4, :].bitcast(I32),
+                )
+
+        offs_t = tile([P, S // 16], U16, "offs_t")
+        ent_t = tile([P, S // 16], U16, "ent_t")
+        xw = tile([P, T], U32, "xw")
+        xs = placed([P, T], U8, "xs", 11264)
+        w1w = placed([P, H], I32, "w1w", 3072)
+        ws = tile([P, H], U8, "ws")
+        gn_t = tile([P, PACK], F32, "gn_t")
+
+        nc.vector.memset(xs[:, 0 : T // 2].bitcast(I32), 0)
+        nc.gpsimd.memset(xs[:, T // 2 : T].bitcast(I32), 0)
+        nc.vector.memset(ws[:].bitcast(I32), 0)
+
+        ef_rows = ef.rearrange("(p t) u -> t p u", t=PACK)
+        nc.sync.dma_start(offs_t[:], offs)
+        nc.sync.dma_start(ent_t[:], ent)
+        nc.sync.dma_start(out=w1w[:], in_=words(w1_words))
+        load_scale_rows(nc.sync, xs, 0, x_scales)
+        nc.sync.dma_start(out=xw[:].bitcast(I32), in_=words(x_words))
+        load_scale_rows(nc.sync, ws, W1_ROW, w1_scales)
+        nc.sync.dma_start(out=gn_t[:], in_=gn.rearrange("(p t) o -> p (t o)", t=PACK))
+
+        ef_t = []
+
+        def load_ef(t):
+            plane = placed([P, U], F32, f"ef{t}", 4096 * t)
+            nc.sync.dma_start(out=plane[:], in_=ef_rows[t])
+            ef_t.append(plane)
+
+        quarter = tile([P, PACK], F32, "quarter")
+        rest = tile([P, PACK], F32, "rest")
+        nc.scalar.activation(quarter[:], gn_t[:], ACT.Copy, scale=0.25)
+        nc.scalar.activation(rest[:], gn_t[:], ACT.Copy, scale=0.75)
+
+        def deal_words(dst, src):
+            nc.vector.tensor_copy(
+                out=dst[:].rearrange("p (t c i) -> p c t i", t=PACK, i=4),
+                in_=src[:].rearrange("p (c i t) -> p c t i", t=PACK, i=4),
+            )
+
+        def deal_bytes(dst, src):
+            nc.vector.tensor_copy(
+                out=dst[:].rearrange("p (t m) -> p t m", t=PACK), in_=src[:].rearrange("p (m t) -> p t m", t=PACK)
+            )
+
+        w1d = tile([P, H], I32, "w1d")
+        deal_words(w1d, w1w)
+        load_ef(0)
+        load_ef(1)
+        xs_g = placed([P, S], U8, "xs_g", 16384)
+        nc.vector.tensor_copy(xs_g[:], xs[:].indirect(offs_t[:]))
+        load_ef(2)
+        load_ef(3)
+        w1sd = tile([P, H], U8, "w1sd")
+
+        y = []
+        for h in range(2):
+            xw_g = tile([P, HALF], U32, f"xw_g{h}")
+            nc.vector.tensor_copy(xw_g[:], xw[:].indirect(offs_t[:, 16 * h : 16 * h + 16]))
+            if h == 0:
+                deal_bytes(w1sd, ws)
+            y_h = tile([P, PACK, HALF], F32, f"y{h}")
+            for u in range(2):
+                bank = ps.tile([P, 2, HALF], F32, name=f"yb{h}{u}")
+                for e in range(2):
+                    t = 2 * u + e
+                    nc.tensor.matmul_mx(
+                        out=bank[:, e, :],
+                        lhsT=w1d[:, P * t : P * (t + 1)].bitcast(FP8X4),
+                        lhsT_scale=w1sd[W1_ROW:P, P * t : P * (t + 1)],
+                        rhs=xw_g[:].bitcast(FP8X4),
+                        rhs_scale=xs_g[:, HALF * h : HALF * (h + 1)],
+                        start=True,
+                        stop=True,
+                    )
+                nc.scalar.copy(out=y_h[:, 2 * u : 2 * u + 2, :], in_=bank[:])
+            y.append(y_h)
+
+        w2w = placed([P, N], I32, "w2w", 16384)
+        nc.sync.dma_start(out=w2w[:], in_=words(w2_words))
+        load_scale_rows(nc.sync, ws, W2_ROW, w2_scales)
+
+        a = [tile([P, PACK, HALF], F32, f"a{h}") for h in range(2)]
+        sent = [tile([P, PACK, HALF], F32, f"sent{h}") for h in range(2)]
+        lin = [tile([P, PACK, HALF], F32, f"lin{h}") for h in range(2)]
+        cut = [tile([P, PACK, HALF], F32, f"cut{h}") for h in range(2)]
+
+        def add_error(h, t):
+            nc.vector.tensor_tensor(
+                a[h][:, t, :], ef_t[t][:].indirect(ent_t[:, 16 * h : 16 * h + 16]), y[h][:, t, :], ALU.add
+            )
+            nc.scalar.activation(lin[h][:, t, :], a[h][:, t, :], ACT.Copy, scale=quarter[:, t : t + 1])
+
+        def clip(h, t):
+            nc.vector.tensor_scalar(sent[h][:, t, :], a[h][:, t, :], 0.5, -0.5, ALU.min, ALU.max)
+            nc.scalar.activation(cut[h][:, t, :], sent[h][:, t, :], ACT.Copy, scale=rest[:, t : t + 1])
+
+        w2d = tile([P, N], I32, "w2d")
+        w2sd = tile([P, N], U8, "w2sd")
+        o_words = tile([P, S], U32, "o_words")
+        o_scales = tile([P, S], U8, "o_scales")
+        out_rows = out_0.rearrange("(p t) j -> p t j", t=PACK)
+        out_words = words(out_1)
+
+        def make_z(c):
+            h, cols = c // 2, slice(CHUNK * (c % 2), CHUNK * (c % 2 + 1))
+            z = tile([P, PACK * CHUNK], BF16, f"z{c}")
+            nc.vector.tensor_tensor(
+                z[:].rearrange("p (c i t) -> p c t i", t=PACK, i=4),
+                lin[h][:, :, cols].rearrange("p t (c i) -> p c t i", i=4),
+                cut[h][:, :, cols].rearrange("p t (c i) -> p c t i", i=4),
+                ALU.add,
+            )
+            return z
+
+        def second_product(c, z):
+            zw = tile([P, CHUNK], U32, f"zw{c}")
+            zs = tile([P, CHUNK], U8, f"zs{c}")
+            nc.vector.quantize_mx(out=zw[:].bitcast(FP8X4), scales=zs[:], in_=z[:])
+            bank = ps.tile([P, PACK, CHUNK], F32, name=f"ob{c}")
+            for t in range(PACK):
+                nc.tensor.matmul_mx(
+                    out=bank[:, t, :],
+                    lhsT=w2d[:, P * t : P * (t + 1)].bitcast(FP8X4),
+                    lhsT_scale=w2sd[W2_ROW:P, P * t : P * (t + 1)],
+                    rhs=zw[:].bitcast(FP8X4),
+                    rhs_scale=zs[:],
+                    start=True,
+                    stop=True,
+                )
+            rounded = tile([P, CHUNK, PACK], BF16, f"rounded{c}")
+            nc.scalar.copy(out=rounded[:], in_=bank[:].rearrange("p t n -> p n t"))
+            res = tile([P, PACK, CHUNK], F32, f"res{c}")
+            nc.scalar.copy(out=res[:], in_=bank[:])
+            nc.sync.dma_start(out=out_rows[:, :, CHUNK * c : CHUNK * (c + 1)], in_=res[:])
+            return rounded
+
+        def hand_on(c, rounded):
+            cols = slice(CHUNK * c, CHUNK * (c + 1))
+            nc.vector.quantize_mx(
+                out=o_words[:, cols].bitcast(FP8X4),
+                scales=o_scales[:, cols],
+                in_=rounded[:].rearrange("p n t -> p (n t)"),
+            )
+
+        for t in range(PACK - 1):
+            add_error(0, t)
+            add_error(1, t)
+            clip(0, t)
+            clip(1, t)
+        add_error(0, 3)
+        deal_words(w2d, w2w)
+        deal_bytes(w2sd, ws)
+        clip(0, 3)
+        add_error(1, 3)
+        z0 = make_z(0)
+        clip(1, 3)
+        z1 = make_z(1)
+        r0 = second_product(0, z0)
+        z2 = make_z(2)
+        r1 = second_product(1, z1)
+        z3 = make_z(3)
+        r2 = second_product(2, z2)
+        hand_on(0, r0)
+        r3 = second_product(3, z3)
+        hand_on(1, r1)
+        nc.sync.dma_start(out=out_words[:, 0:HALF], in_=o_words[:, 0:HALF].bitcast(I32))
+        hand_on(2, r2)
+        hand_on(3, r3)
+        nc.sync.dma_start(out=out_words[:, HALF:S], in_=o_words[:, HALF:S].bitcast(I32))
+        for q in range(4):
+            eng = nc.sync if q % 2 else nc.scalar
+            eng.dma_start(
+                out=out_2[0, 4 * q : 4 * q + 4, :].bitcast(I32), in_=o_scales[32 * q : 32 * q + 4, :].bitcast(I32)
+            )

@@ -50,7 +50,7 @@ def tile_picked_errfb_none_po_kernel(
 
         offs_t = tile([P, S // 16], U16, "offs_t")
         ent_t = tile([P, S // 16], U16, "ent_t")
-        xw = tile([P, T], U32, "xw")
+        xw = placed([P, T], U32, "xw", 16384)
         xs = placed([P, T], U8, "xs", 11264)
         w1w = placed([P, H], I32, "w1w", 3072)
         ws = tile([P, H], U8, "ws")
@@ -96,69 +96,81 @@ def tile_picked_errfb_none_po_kernel(
         deal_words(w1d, w1w)
         load_ef(0)
         load_ef(1)
-        xs_g = placed([P, S], U8, "xs_g", 16384)
+        xs_g = tile([P, S], U8, "xs_g")
         nc.vector.tensor_copy(xs_g[:], xs[:].indirect(offs_t[:]))
         load_ef(2)
         load_ef(3)
+        xw_g = tile([P, S], U32, "xw_g")
+        nc.vector.tensor_copy(xw_g[:], xw[:].indirect(offs_t[:]))
         w1sd = tile([P, H], U8, "w1sd")
-
-        y = []
-        for h in range(2):
-            xw_g = tile([P, HALF], U32, f"xw_g{h}")
-            nc.vector.tensor_copy(xw_g[:], xw[:].indirect(offs_t[:, 16 * h : 16 * h + 16]))
-            if h == 0:
-                deal_bytes(w1sd, ws)
-            y_h = tile([P, PACK, HALF], F32, f"y{h}")
-            for u in range(2):
-                bank = ps.tile([P, 2, HALF], F32, name=f"yb{h}{u}")
-                for e in range(2):
-                    t = 2 * u + e
-                    nc.tensor.matmul_mx(
-                        out=bank[:, e, :],
-                        lhsT=w1d[:, P * t : P * (t + 1)].bitcast(FP8X4),
-                        lhsT_scale=w1sd[W1_ROW:P, P * t : P * (t + 1)],
-                        rhs=xw_g[:].bitcast(FP8X4),
-                        rhs_scale=xs_g[:, HALF * h : HALF * (h + 1)],
-                        start=True,
-                        stop=True,
-                    )
-                nc.scalar.copy(out=y_h[:, 2 * u : 2 * u + 2, :], in_=bank[:])
-            y.append(y_h)
-
+        deal_bytes(w1sd, ws)
         w2w = placed([P, N], I32, "w2w", 16384)
         nc.sync.dma_start(out=w2w[:], in_=words(w2_words))
         load_scale_rows(nc.sync, ws, W2_ROW, w2_scales)
 
-        a = [tile([P, PACK, HALF], F32, f"a{h}") for h in range(2)]
-        sent = [tile([P, PACK, HALF], F32, f"sent{h}") for h in range(2)]
-        lin = [tile([P, PACK, HALF], F32, f"lin{h}") for h in range(2)]
-        cut = [tile([P, PACK, HALF], F32, f"cut{h}") for h in range(2)]
-
-        def add_error(h, t):
-            nc.vector.tensor_tensor(
-                a[h][:, t, :], ef_t[t][:].indirect(ent_t[:, 16 * h : 16 * h + 16]), y[h][:, t, :], ALU.add
+        y_ps = []
+        for t in range(PACK):
+            bank = ps.tile([P, S], F32, name=f"y_ps{t}")
+            nc.tensor.matmul_mx(
+                out=bank[:],
+                lhsT=w1d[:, P * t : P * (t + 1)].bitcast(FP8X4),
+                lhsT_scale=w1sd[W1_ROW:P, P * t : P * (t + 1)],
+                rhs=xw_g[:].bitcast(FP8X4),
+                rhs_scale=xs_g[:],
+                start=True,
+                stop=True,
             )
-            nc.scalar.activation(lin[h][:, t, :], a[h][:, t, :], ACT.Copy, scale=quarter[:, t : t + 1])
+            y_ps.append(bank)
+        y = {}
+        for t in range(1, PACK):
+            y[t] = tile([P, S], F32, f"y{t}")
+            nc.scalar.copy(out=y[t][:], in_=y_ps[t][:])
 
-        def clip(h, t):
-            nc.vector.tensor_scalar(sent[h][:, t, :], a[h][:, t, :], 0.5, -0.5, ALU.min, ALU.max)
-            nc.scalar.activation(cut[h][:, t, :], sent[h][:, t, :], ACT.Copy, scale=rest[:, t : t + 1])
+        a = tile([P, PACK, S], F32, "a")
+        sent = tile([P, PACK, S], F32, "sent")
+        lin = tile([P, PACK, S], F32, "lin")
+        cut = tile([P, PACK, S], F32, "cut")
+        halves = [slice(0, HALF), slice(HALF, S)]
+        ent_half = [ent_t[:, 0:16], ent_t[:, 16:32]]
 
-        w2d = tile([P, N], I32, "w2d")
-        w2sd = tile([P, N], U8, "w2sd")
+        kept = tile([P, S], F32, "kept")
+        for h, cols in enumerate(halves):
+            nc.vector.tensor_copy(kept[:, cols], ef_t[0][:].indirect(ent_half[h]))
+
+        for t in range(PACK):
+            for h, cols in enumerate(halves):
+                if t == 0:
+                    nc.vector.tensor_tensor(a[:, 0, cols], y_ps[0][:, cols], kept[:, cols], ALU.add)
+                else:
+                    nc.vector.tensor_tensor(a[:, t, cols], ef_t[t][:].indirect(ent_half[h]), y[t][:, cols], ALU.add)
+                nc.scalar.activation(lin[:, t, cols], a[:, t, cols], ACT.Copy, scale=quarter[:, t : t + 1])
+            for cols in halves:
+                nc.vector.tensor_scalar(sent[:, t, cols], a[:, t, cols], 0.5, -0.5, ALU.min, ALU.max)
+                nc.scalar.activation(cut[:, t, cols], sent[:, t, cols], ACT.Copy, scale=rest[:, t : t + 1])
+
+        w2d = placed([P, N], I32, "w2d", 12288)
+        w2sd = placed([P, N], U8, "w2sd", 14336)
+        deal_words(w2d, w2w)
+        deal_bytes(w2sd, ws)
+
         o_words = tile([P, S], U32, "o_words")
         o_scales = tile([P, S], U8, "o_scales")
         out_rows = out_0.rearrange("(p t) j -> p t j", t=PACK)
         out_words = words(out_1)
 
+        def woven_view(woven):
+            return woven[:].rearrange("p (c i t) -> p c t i", t=PACK, i=4)
+
+        def planes_view(planes):
+            return planes.rearrange("p t (c i) -> p c t i", i=4)
+
+        def chunk(c):
+            return slice(CHUNK * c, CHUNK * (c + 1))
+
         def make_z(c):
-            h, cols = c // 2, slice(CHUNK * (c % 2), CHUNK * (c % 2 + 1))
             z = tile([P, PACK * CHUNK], BF16, f"z{c}")
             nc.vector.tensor_tensor(
-                z[:].rearrange("p (c i t) -> p c t i", t=PACK, i=4),
-                lin[h][:, :, cols].rearrange("p t (c i) -> p c t i", i=4),
-                cut[h][:, :, cols].rearrange("p t (c i) -> p c t i", i=4),
-                ALU.add,
+                woven_view(z), planes_view(lin[:, :, chunk(c)]), planes_view(cut[:, :, chunk(c)]), ALU.add
             )
             return z
 
@@ -166,7 +178,7 @@ def tile_picked_errfb_none_po_kernel(
             zw = tile([P, CHUNK], U32, f"zw{c}")
             zs = tile([P, CHUNK], U8, f"zs{c}")
             nc.vector.quantize_mx(out=zw[:].bitcast(FP8X4), scales=zs[:], in_=z[:])
-            bank = ps.tile([P, PACK, CHUNK], F32, name=f"ob{c}")
+            bank = ps.tile([P, PACK, CHUNK], F32, name=f"o_ps{c}")
             for t in range(PACK):
                 nc.tensor.matmul_mx(
                     out=bank[:, t, :],
@@ -177,43 +189,36 @@ def tile_picked_errfb_none_po_kernel(
                     start=True,
                     stop=True,
                 )
-            rounded = tile([P, CHUNK, PACK], BF16, f"rounded{c}")
-            nc.scalar.copy(out=rounded[:], in_=bank[:].rearrange("p t n -> p n t"))
             res = tile([P, PACK, CHUNK], F32, f"res{c}")
             nc.scalar.copy(out=res[:], in_=bank[:])
-            nc.sync.dma_start(out=out_rows[:, :, CHUNK * c : CHUNK * (c + 1)], in_=res[:])
+            nc.sync.dma_start(out=out_rows[:, :, chunk(c)], in_=res[:])
+            return res
+
+        def round_result(c, res):
+            rounded = tile([P, PACK * CHUNK], BF16, f"rounded{c}")
+            nc.vector.tensor_copy(out=woven_view(rounded), in_=planes_view(res[:]))
             return rounded
 
         def hand_on(c, rounded):
-            cols = slice(CHUNK * c, CHUNK * (c + 1))
             nc.vector.quantize_mx(
-                out=o_words[:, cols].bitcast(FP8X4),
-                scales=o_scales[:, cols],
-                in_=rounded[:].rearrange("p n t -> p (n t)"),
+                out=o_words[:, chunk(c)].bitcast(FP8X4), scales=o_scales[:, chunk(c)], in_=rounded[:]
             )
 
-        for t in range(PACK - 1):
-            add_error(0, t)
-            add_error(1, t)
-            clip(0, t)
-            clip(1, t)
-        add_error(0, 3)
-        deal_words(w2d, w2w)
-        deal_bytes(w2sd, ws)
-        clip(0, 3)
-        add_error(1, 3)
         z0 = make_z(0)
-        clip(1, 3)
         z1 = make_z(1)
-        r0 = second_product(0, z0)
+        res0 = second_product(0, z0)
         z2 = make_z(2)
-        r1 = second_product(1, z1)
+        res1 = second_product(1, z1)
         z3 = make_z(3)
-        r2 = second_product(2, z2)
+        res2 = second_product(2, z2)
+        res3 = second_product(3, z3)
+        r0 = round_result(0, res0)
+        r1 = round_result(1, res1)
         hand_on(0, r0)
-        r3 = second_product(3, z3)
+        r2 = round_result(2, res2)
         hand_on(1, r1)
         nc.sync.dma_start(out=out_words[:, 0:HALF], in_=o_words[:, 0:HALF].bitcast(I32))
+        r3 = round_result(3, res3)
         hand_on(2, r2)
         hand_on(3, r3)
         nc.sync.dma_start(out=out_words[:, HALF:S], in_=o_words[:, HALF:S].bitcast(I32))

@@ -83,8 +83,8 @@ def tile_picked_errfb_none_po_kernel(
 
         def deal_words(dst, src):
             nc.vector.tensor_copy(
-                out=dst[:].rearrange("p (t c i) -> p c t i", t=PACK, i=4),
-                in_=src[:].rearrange("p (c i t) -> p c t i", t=PACK, i=4),
+                out=dst[:].rearrange("p (u e c i) -> p c u i e", u=2, e=2, i=4),
+                in_=src[:].rearrange("p (c i u e) -> p c u i e", u=2, e=2, i=4),
             )
 
         def deal_bytes(dst, src):
@@ -155,14 +155,16 @@ def tile_picked_errfb_none_po_kernel(
 
         o_words = tile([P, S], U32, "o_words")
         o_scales = tile([P, S], U8, "o_scales")
+        res = tile([P, PACK, S], F32, "res")
+        rounded = tile([P, PACK * S], BF16, "rounded")
         out_rows = out_0.rearrange("(p t) j -> p t j", t=PACK)
         out_words = words(out_1)
 
         def woven_view(woven):
-            return woven[:].rearrange("p (c i t) -> p c t i", t=PACK, i=4)
+            return woven.rearrange("p (c i t) -> p c t i", t=PACK, i=2)
 
         def planes_view(planes):
-            return planes.rearrange("p t (c i) -> p c t i", i=4)
+            return planes.rearrange("p t (c i) -> p c t i", i=2)
 
         def chunk(c):
             return slice(CHUNK * c, CHUNK * (c + 1))
@@ -170,7 +172,7 @@ def tile_picked_errfb_none_po_kernel(
         def make_z(c):
             z = tile([P, PACK * CHUNK], BF16, f"z{c}")
             nc.vector.tensor_tensor(
-                woven_view(z), planes_view(lin[:, :, chunk(c)]), planes_view(cut[:, :, chunk(c)]), ALU.add
+                woven_view(z[:]), planes_view(lin[:, :, chunk(c)]), planes_view(cut[:, :, chunk(c)]), ALU.add
             )
             return z
 
@@ -189,41 +191,45 @@ def tile_picked_errfb_none_po_kernel(
                     start=True,
                     stop=True,
                 )
-            res = tile([P, PACK, CHUNK], F32, f"res{c}")
-            nc.scalar.copy(out=res[:], in_=bank[:])
-            nc.sync.dma_start(out=out_rows[:, :, chunk(c)], in_=res[:])
-            return res
+            nc.scalar.copy(out=res[:, :, chunk(c)], in_=bank[:])
 
-        def round_result(c, res):
-            rounded = tile([P, PACK * CHUNK], BF16, f"rounded{c}")
-            nc.vector.tensor_copy(out=woven_view(rounded), in_=planes_view(res[:]))
-            return rounded
+        def store_result(cols):
+            nc.sync.dma_start(out=out_rows[:, :, cols], in_=res[:, :, cols])
 
-        def hand_on(c, rounded):
+        def round_result(cols):
+            nc.vector.tensor_copy(
+                out=woven_view(rounded[:, PACK * cols.start : PACK * cols.stop]), in_=planes_view(res[:, :, cols])
+            )
+
+        def hand_on(cols):
             nc.vector.quantize_mx(
-                out=o_words[:, chunk(c)].bitcast(FP8X4), scales=o_scales[:, chunk(c)], in_=rounded[:]
+                out=o_words[:, cols].bitcast(FP8X4),
+                scales=o_scales[:, cols],
+                in_=rounded[:, PACK * cols.start : PACK * cols.stop],
             )
 
         z0 = make_z(0)
         z1 = make_z(1)
-        res0 = second_product(0, z0)
+        second_product(0, z0)
         z2 = make_z(2)
-        res1 = second_product(1, z1)
+        second_product(1, z1)
+        store_result(halves[0])
         z3 = make_z(3)
-        res2 = second_product(2, z2)
-        res3 = second_product(3, z3)
-        r0 = round_result(0, res0)
-        r1 = round_result(1, res1)
-        hand_on(0, r0)
-        r2 = round_result(2, res2)
-        hand_on(1, r1)
-        nc.sync.dma_start(out=out_words[:, 0:HALF], in_=o_words[:, 0:HALF].bitcast(I32))
-        r3 = round_result(3, res3)
-        hand_on(2, r2)
-        hand_on(3, r3)
-        nc.sync.dma_start(out=out_words[:, HALF:S], in_=o_words[:, HALF:S].bitcast(I32))
+        second_product(2, z2)
+        store_result(chunk(2))
+        second_product(3, z3)
+        store_result(chunk(3))
+        round_result(halves[0])
+        round_result(chunk(2))
+        hand_on(halves[0])
+        round_result(chunk(3))
+        hand_on(chunk(2))
+        early = slice(0, S - CHUNK)
+        nc.sync.dma_start(out=out_words[:, early], in_=o_words[:, early].bitcast(I32))
+        hand_on(chunk(3))
+        nc.scalar.dma_start(out=out_words[:, chunk(3)], in_=o_words[:, chunk(3)].bitcast(I32))
         for q in range(4):
-            eng = nc.sync if q % 2 else nc.scalar
+            eng = nc.scalar if q % 2 else nc.sync
             eng.dma_start(
                 out=out_2[0, 4 * q : 4 * q + 4, :].bitcast(I32), in_=o_scales[32 * q : 32 * q + 4, :].bitcast(I32)
             )

@@ -17,10 +17,18 @@ ACT = mybir.ActivationFunctionType
 
 P = 128
 PACK = 4
-HALF = 256
-CHUNK = 128
+QUADRANT = 32
+GROUP = 16
+HALF = S // 2
+CHUNK = S // 4
 W1_ROW = 4
 W2_ROW = 8
+
+EF_BYTES = 4 * U
+W1_WORDS_AT = EF_BYTES - 2 * H
+X_SCALES_AT = 3 * EF_BYTES - T // 2
+X_WORDS_AT = PACK * EF_BYTES
+W2_DEALT_AT = 3 * EF_BYTES
 
 
 def tile_picked_errfb_none_po_kernel(
@@ -41,18 +49,20 @@ def tile_picked_errfb_none_po_kernel(
         def words(dram):
             return dram[0].rearrange("p n t -> p (n t)").bitcast(I32)
 
-        def load_scale_rows(queue, plane, first, dram):
+        def load_scale_rows(scale_tile, first, dram):
             for q in range(4):
-                queue.dma_start(
-                    out=plane[32 * q + first : 32 * q + first + 4, :].bitcast(I32),
+                nc.sync.dma_start(
+                    out=scale_tile[QUADRANT * q + first : QUADRANT * q + first + 4, :].bitcast(I32),
                     in_=dram[0, 4 * q : 4 * q + 4, :].bitcast(I32),
                 )
 
-        offs_t = tile([P, S // 16], U16, "offs_t")
-        ent_t = tile([P, S // 16], U16, "ent_t")
-        xw = placed([P, T], U32, "xw", 16384)
-        xs = placed([P, T], U8, "xs", 11264)
-        w1w = placed([P, H], I32, "w1w", 3072)
+        halves = [slice(0, HALF), slice(HALF, S)]
+
+        offs_t = tile([P, S // GROUP], U16, "offs_t")
+        ent_t = tile([P, S // GROUP], U16, "ent_t")
+        xw = placed([P, T], U32, "xw", X_WORDS_AT)
+        xs = placed([P, T], U8, "xs", X_SCALES_AT)
+        w1w = placed([P, H], I32, "w1w", W1_WORDS_AT)
         ws = tile([P, H], U8, "ws")
         gn_t = tile([P, PACK], F32, "gn_t")
 
@@ -64,15 +74,15 @@ def tile_picked_errfb_none_po_kernel(
         nc.sync.dma_start(offs_t[:], offs)
         nc.sync.dma_start(ent_t[:], ent)
         nc.sync.dma_start(out=w1w[:], in_=words(w1_words))
-        load_scale_rows(nc.sync, xs, 0, x_scales)
+        load_scale_rows(xs, 0, x_scales)
         nc.sync.dma_start(out=xw[:].bitcast(I32), in_=words(x_words))
-        load_scale_rows(nc.sync, ws, W1_ROW, w1_scales)
+        load_scale_rows(ws, W1_ROW, w1_scales)
         nc.sync.dma_start(out=gn_t[:], in_=gn.rearrange("(p t) o -> p (t o)", t=PACK))
 
         ef_t = []
 
         def load_ef(t):
-            plane = placed([P, U], F32, f"ef{t}", 4096 * t)
+            plane = placed([P, U], F32, f"ef{t}", EF_BYTES * t)
             nc.sync.dma_start(out=plane[:], in_=ef_rows[t])
             ef_t.append(plane)
 
@@ -104,9 +114,9 @@ def tile_picked_errfb_none_po_kernel(
         nc.vector.tensor_copy(xw_g[:], xw[:].indirect(offs_t[:]))
         w1sd = tile([P, H], U8, "w1sd")
         deal_bytes(w1sd, ws)
-        w2w = placed([P, N], I32, "w2w", 16384)
+        w2w = placed([P, N], I32, "w2w", X_WORDS_AT)
         nc.sync.dma_start(out=w2w[:], in_=words(w2_words))
-        load_scale_rows(nc.sync, ws, W2_ROW, w2_scales)
+        load_scale_rows(ws, W2_ROW, w2_scales)
 
         y_ps = []
         for t in range(PACK):
@@ -121,17 +131,18 @@ def tile_picked_errfb_none_po_kernel(
                 stop=True,
             )
             y_ps.append(bank)
+
         y = {}
         for t in range(1, PACK):
             y[t] = tile([P, S], F32, f"y{t}")
-            nc.scalar.copy(out=y[t][:], in_=y_ps[t][:])
+            for cols in halves if t == 1 else [slice(0, S)]:
+                nc.scalar.copy(out=y[t][:, cols], in_=y_ps[t][:, cols])
 
         a = tile([P, PACK, S], F32, "a")
         sent = tile([P, PACK, S], F32, "sent")
         lin = tile([P, PACK, S], F32, "lin")
         cut = tile([P, PACK, S], F32, "cut")
-        halves = [slice(0, HALF), slice(HALF, S)]
-        ent_half = [ent_t[:, 0:16], ent_t[:, 16:32]]
+        ent_half = [ent_t[:, cols.start // GROUP : cols.stop // GROUP] for cols in halves]
 
         kept = tile([P, S], F32, "kept")
         for h, cols in enumerate(halves):
@@ -148,8 +159,8 @@ def tile_picked_errfb_none_po_kernel(
                 nc.vector.tensor_scalar(sent[:, t, cols], a[:, t, cols], 0.5, -0.5, ALU.min, ALU.max)
                 nc.scalar.activation(cut[:, t, cols], sent[:, t, cols], ACT.Copy, scale=rest[:, t : t + 1])
 
-        w2d = placed([P, N], I32, "w2d", 12288)
-        w2sd = placed([P, N], U8, "w2sd", 14336)
+        w2d = placed([P, N], I32, "w2d", W2_DEALT_AT)
+        w2sd = placed([P, N], U8, "w2sd", W2_DEALT_AT + 4 * N)
         deal_words(w2d, w2w)
         deal_bytes(w2sd, ws)
 
@@ -168,6 +179,9 @@ def tile_picked_errfb_none_po_kernel(
 
         def chunk(c):
             return slice(CHUNK * c, CHUNK * (c + 1))
+
+        def woven_columns(cols):
+            return slice(PACK * cols.start, PACK * cols.stop)
 
         def make_z(c):
             z = tile([P, PACK * CHUNK], BF16, f"z{c}")
@@ -192,44 +206,35 @@ def tile_picked_errfb_none_po_kernel(
                     stop=True,
                 )
             nc.scalar.copy(out=res[:, :, chunk(c)], in_=bank[:])
-
-        def store_result(cols):
-            nc.sync.dma_start(out=out_rows[:, :, cols], in_=res[:, :, cols])
+            nc.sync.dma_start(out=out_rows[:, :, chunk(c)], in_=res[:, :, chunk(c)])
 
         def round_result(cols):
-            nc.vector.tensor_copy(
-                out=woven_view(rounded[:, PACK * cols.start : PACK * cols.stop]), in_=planes_view(res[:, :, cols])
-            )
+            nc.vector.tensor_copy(out=woven_view(rounded[:, woven_columns(cols)]), in_=planes_view(res[:, :, cols]))
 
         def hand_on(cols):
             nc.vector.quantize_mx(
-                out=o_words[:, cols].bitcast(FP8X4),
-                scales=o_scales[:, cols],
-                in_=rounded[:, PACK * cols.start : PACK * cols.stop],
+                out=o_words[:, cols].bitcast(FP8X4), scales=o_scales[:, cols], in_=rounded[:, woven_columns(cols)]
             )
 
-        z0 = make_z(0)
-        z1 = make_z(1)
-        second_product(0, z0)
-        z2 = make_z(2)
-        second_product(1, z1)
-        store_result(halves[0])
-        z3 = make_z(3)
-        second_product(2, z2)
-        store_result(chunk(2))
-        second_product(3, z3)
-        store_result(chunk(3))
-        round_result(halves[0])
-        round_result(chunk(2))
-        hand_on(halves[0])
-        round_result(chunk(3))
-        hand_on(chunk(2))
-        early = slice(0, S - CHUNK)
-        nc.sync.dma_start(out=out_words[:, early], in_=o_words[:, early].bitcast(I32))
-        hand_on(chunk(3))
-        nc.scalar.dma_start(out=out_words[:, chunk(3)], in_=o_words[:, chunk(3)].bitcast(I32))
+        chunks = S // CHUNK
+        ahead = make_z(0)
+        for c in range(chunks):
+            z_now = ahead
+            if c + 1 < chunks:
+                ahead = make_z(c + 1)
+            second_product(c, z_now)
+
+        pieces = [halves[0], chunk(2), chunk(3)]
+        round_result(pieces[0])
+        for k, cols in enumerate(pieces):
+            if k + 1 < len(pieces):
+                round_result(pieces[k + 1])
+            hand_on(cols)
+
+        nc.sync.dma_start(out=out_words, in_=o_words[:].bitcast(I32))
         for q in range(4):
-            eng = nc.scalar if q % 2 else nc.sync
-            eng.dma_start(
-                out=out_2[0, 4 * q : 4 * q + 4, :].bitcast(I32), in_=o_scales[32 * q : 32 * q + 4, :].bitcast(I32)
+            queue = nc.sync if q == 3 else nc.scalar
+            queue.dma_start(
+                out=out_2[0, 4 * q : 4 * q + 4, :].bitcast(I32),
+                in_=o_scales[QUADRANT * q : QUADRANT * q + 4, :].bitcast(I32),
             )

@@ -66,8 +66,7 @@ def tile_picked_errfb_none_po_kernel(
         ws = tile([P, H], U8, "ws")
         gn_t = tile([P, PACK], F32, "gn_t")
 
-        nc.vector.memset(xs[:, 0 : T // 2].bitcast(I32), 0)
-        nc.gpsimd.memset(xs[:, T // 2 : T].bitcast(I32), 0)
+        nc.vector.memset(xs[:].bitcast(I32), 0)
         nc.vector.memset(ws[:].bitcast(I32), 0)
 
         ef_rows = ef.rearrange("(p t) u -> t p u", t=PACK)

@@ -25,10 +25,7 @@ W1_ROW = 4
 W2_ROW = 8
 
 EF_BYTES = 4 * U
-W1_WORDS_AT = EF_BYTES - 2 * H
-X_SCALES_AT = 3 * EF_BYTES - T // 2
-X_WORDS_AT = PACK * EF_BYTES
-W2_DEALT_AT = 3 * EF_BYTES
+W1_SCALES_AT = PACK * EF_BYTES
 
 
 def tile_picked_errfb_none_po_kernel(
@@ -60,35 +57,38 @@ def tile_picked_errfb_none_po_kernel(
 
         offs_t = tile([P, S // GROUP], U16, "offs_t")
         ent_t = tile([P, S // GROUP], U16, "ent_t")
-        xw = placed([P, T], U32, "xw", X_WORDS_AT)
-        xs = placed([P, T], U8, "xs", X_SCALES_AT)
-        w1w = placed([P, H], I32, "w1w", W1_WORDS_AT)
-        ws = tile([P, H], U8, "ws")
+        xw = tile([P, T], U32, "xw")
+        xs = tile([P, T], U8, "xs")
+        w1w = tile([P, H], I32, "w1w")
+        w2w = tile([P, N], I32, "w2w")
+        w1s = placed([P, H], U8, "w1s", W1_SCALES_AT)
+        w2s = tile([P, N], U8, "w2s")
         gn_t = tile([P, PACK], F32, "gn_t")
+        ef_t = [placed([P, U], F32, f"ef{t}", EF_BYTES * t) for t in range(PACK)]
 
         nc.vector.memset(xs[:].bitcast(I32), 0)
-        nc.vector.memset(ws[:].bitcast(I32), 0)
+        nc.vector.memset(w1s[:].bitcast(I32), 0)
+        nc.vector.memset(w2s[:].bitcast(I32), 0)
 
         ef_rows = ef.rearrange("(p t) u -> t p u", t=PACK)
         nc.sync.dma_start(offs_t[:], offs)
-        nc.sync.dma_start(ent_t[:], ent)
+        nc.sync.dma_start(out=gn_t[:], in_=gn.rearrange("(p t) o -> p (t o)", t=PACK))
         nc.sync.dma_start(out=w1w[:], in_=words(w1_words))
         load_scale_rows(xs, 0, x_scales)
         nc.sync.dma_start(out=xw[:].bitcast(I32), in_=words(x_words))
-        load_scale_rows(ws, W1_ROW, w1_scales)
-        nc.sync.dma_start(out=gn_t[:], in_=gn.rearrange("(p t) o -> p (t o)", t=PACK))
-
-        ef_t = []
-
-        def load_ef(t):
-            plane = placed([P, U], F32, f"ef{t}", EF_BYTES * t)
-            nc.sync.dma_start(out=plane[:], in_=ef_rows[t])
-            ef_t.append(plane)
+        load_scale_rows(w1s, W1_ROW, w1_scales)
+        nc.sync.dma_start(ent_t[:], ent)
+        nc.sync.dma_start(out=w2w[:], in_=words(w2_words))
+        for t in range(PACK):
+            nc.sync.dma_start(out=ef_t[t][:], in_=ef_rows[t])
+        load_scale_rows(w2s, W2_ROW, w2_scales)
 
         quarter = tile([P, PACK], F32, "quarter")
-        rest = tile([P, PACK], F32, "rest")
+        high = tile([P, PACK], F32, "high")
+        low = tile([P, PACK], F32, "low")
         nc.scalar.activation(quarter[:], gn_t[:], ACT.Copy, scale=0.25)
-        nc.scalar.activation(rest[:], gn_t[:], ACT.Copy, scale=0.75)
+        nc.scalar.activation(high[:], gn_t[:], ACT.Abs, scale=0.125)
+        nc.scalar.activation(low[:], high[:], ACT.Copy, scale=-1.0)
 
         def deal_words(dst, src):
             nc.vector.tensor_copy(
@@ -101,67 +101,68 @@ def tile_picked_errfb_none_po_kernel(
                 out=dst[:].rearrange("p (t m) -> p t m", t=PACK), in_=src[:].rearrange("p (m t) -> p t m", t=PACK)
             )
 
+        def list_half(list_tile, cols):
+            return list_tile[:, cols.start // GROUP : cols.stop // GROUP]
+
         w1d = tile([P, H], I32, "w1d")
         deal_words(w1d, w1w)
-        load_ef(0)
-        load_ef(1)
         xs_g = tile([P, S], U8, "xs_g")
         nc.vector.tensor_copy(xs_g[:], xs[:].indirect(offs_t[:]))
-        load_ef(2)
-        load_ef(3)
-        xw_g = tile([P, S], U32, "xw_g")
-        nc.vector.tensor_copy(xw_g[:], xw[:].indirect(offs_t[:]))
+        xw_g = [tile([P, HALF], U32, "xw_g0"), placed([P, HALF], U32, "xw_g1", W1_SCALES_AT)]
+        nc.vector.tensor_copy(xw_g[0][:], xw[:].indirect(list_half(offs_t, halves[0])))
         w1sd = tile([P, H], U8, "w1sd")
-        deal_bytes(w1sd, ws)
-        w2w = placed([P, N], I32, "w2w", X_WORDS_AT)
-        nc.sync.dma_start(out=w2w[:], in_=words(w2_words))
-        load_scale_rows(ws, W2_ROW, w2_scales)
+        deal_bytes(w1sd, w1s)
+        nc.vector.tensor_copy(xw_g[1][:], xw[:].indirect(list_half(offs_t, halves[1])))
+        w2d = tile([P, N], I32, "w2d")
+        deal_words(w2d, w2w)
 
-        y_ps = []
-        for t in range(PACK):
-            bank = ps.tile([P, S], F32, name=f"y_ps{t}")
+        a = tile([P, PACK, S], F32, "a")
+        lin = tile([P, PACK, S], F32, "lin")
+        cut = tile([P, PACK, S], F32, "cut")
+        y = tile([P, PACK + 1, HALF], F32, "y")
+
+        def y_half(t, h):
+            if t > 0 and h == 0:
+                return cut[:, t - 1, halves[0]]
+            return y[:, t + h, :]
+
+        def first_product(out, t, h):
             nc.tensor.matmul_mx(
-                out=bank[:],
+                out=out,
                 lhsT=w1d[:, P * t : P * (t + 1)].bitcast(FP8X4),
                 lhsT_scale=w1sd[W1_ROW:P, P * t : P * (t + 1)],
-                rhs=xw_g[:].bitcast(FP8X4),
-                rhs_scale=xs_g[:],
+                rhs=xw_g[h][:].bitcast(FP8X4),
+                rhs_scale=xs_g[:, halves[h]],
                 start=True,
                 stop=True,
             )
-            y_ps.append(bank)
 
-        y = {}
-        for t in range(1, PACK):
-            y[t] = tile([P, S], F32, f"y{t}")
-            for cols in halves if t == 1 else [slice(0, S)]:
-                nc.scalar.copy(out=y[t][:, cols], in_=y_ps[t][:, cols])
+        for t in range(PACK):
+            for h in range(2):
+                bank = ps.tile([P, HALF], F32, name=f"y_ps{t}{h}", tag=f"bank{2 * t + h}")
+                first_product(bank[:], t, h)
+                nc.scalar.copy(out=y_half(t, h), in_=bank[:])
 
-        a = tile([P, PACK, S], F32, "a")
-        sent = tile([P, PACK, S], F32, "sent")
-        lin = tile([P, PACK, S], F32, "lin")
-        cut = tile([P, PACK, S], F32, "cut")
-        ent_half = [ent_t[:, cols.start // GROUP : cols.stop // GROUP] for cols in halves]
+        whole = slice(0, S)
 
-        kept = tile([P, S], F32, "kept")
-        for h, cols in enumerate(halves):
-            nc.vector.tensor_copy(kept[:, cols], ef_t[0][:].indirect(ent_half[h]))
+        def clip(t, cols):
+            nc.vector.tensor_scalar(
+                cut[:, t, cols], lin[:, t, cols], high[:, t : t + 1], low[:, t : t + 1], ALU.min, ALU.max
+            )
 
         for t in range(PACK):
             for h, cols in enumerate(halves):
-                if t == 0:
-                    nc.vector.tensor_tensor(a[:, 0, cols], y_ps[0][:, cols], kept[:, cols], ALU.add)
-                else:
-                    nc.vector.tensor_tensor(a[:, t, cols], ef_t[t][:].indirect(ent_half[h]), y[t][:, cols], ALU.add)
+                nc.vector.tensor_tensor(
+                    a[:, t, cols], ef_t[t][:].indirect(list_half(ent_t, cols)), y_half(t, h), ALU.add
+                )
+            for cols in halves if t == PACK - 1 else [whole]:
                 nc.scalar.activation(lin[:, t, cols], a[:, t, cols], ACT.Copy, scale=quarter[:, t : t + 1])
-            for cols in halves:
-                nc.vector.tensor_scalar(sent[:, t, cols], a[:, t, cols], 0.5, -0.5, ALU.min, ALU.max)
-                nc.scalar.activation(cut[:, t, cols], sent[:, t, cols], ACT.Copy, scale=rest[:, t : t + 1])
+            if t > 0:
+                clip(t - 1, whole)
 
-        w2d = placed([P, N], I32, "w2d", W2_DEALT_AT)
-        w2sd = placed([P, N], U8, "w2sd", W2_DEALT_AT + 4 * N)
-        deal_words(w2d, w2w)
-        deal_bytes(w2sd, ws)
+        w2sd = placed([P, N], U8, "w2sd", EF_BYTES * (PACK - 1))
+        clip(PACK - 1, halves[0])
+        deal_bytes(w2sd, w2s)
 
         o_words = tile([P, S], U32, "o_words")
         o_scales = tile([P, S], U8, "o_scales")
@@ -184,27 +185,37 @@ def tile_picked_errfb_none_po_kernel(
 
         def make_z(c):
             z = tile([P, PACK * CHUNK], BF16, f"z{c}")
-            nc.vector.tensor_tensor(
-                woven_view(z[:]), planes_view(lin[:, :, chunk(c)]), planes_view(cut[:, :, chunk(c)]), ALU.add
+            nc.vector.scalar_tensor_tensor(
+                z[:].rearrange("p (j t) -> p j t", t=PACK),
+                cut[:, :, chunk(c)].rearrange("p t j -> p j t"),
+                3.0,
+                lin[:, :, chunk(c)].rearrange("p t j -> p j t"),
+                ALU.mult,
+                ALU.add,
             )
             return z
 
-        def second_product(c, z):
+        def quantise_z(c, z):
             zw = tile([P, CHUNK], U32, f"zw{c}")
             zs = tile([P, CHUNK], U8, f"zs{c}")
             nc.vector.quantize_mx(out=zw[:].bitcast(FP8X4), scales=zs[:], in_=z[:])
-            bank = ps.tile([P, PACK, CHUNK], F32, name=f"o_ps{c}")
-            for t in range(PACK):
-                nc.tensor.matmul_mx(
-                    out=bank[:, t, :],
-                    lhsT=w2d[:, P * t : P * (t + 1)].bitcast(FP8X4),
-                    lhsT_scale=w2sd[W2_ROW:P, P * t : P * (t + 1)],
-                    rhs=zw[:].bitcast(FP8X4),
-                    rhs_scale=zs[:],
-                    start=True,
-                    stop=True,
-                )
-            nc.scalar.copy(out=res[:, :, chunk(c)], in_=bank[:])
+            return zw, zs
+
+        def second_product(c, z, groups):
+            zw, zs = quantise_z(c, z)
+            for g, planes in enumerate(groups):
+                bank = ps.tile([P, len(planes), CHUNK], F32, name=f"o_ps{c}{g}", tag=f"bank{c + g}")
+                for k, t in enumerate(planes):
+                    nc.tensor.matmul_mx(
+                        out=bank[:, k, :],
+                        lhsT=w2d[:, P * t : P * (t + 1)].bitcast(FP8X4),
+                        lhsT_scale=w2sd[W2_ROW:P, P * t : P * (t + 1)],
+                        rhs=zw[:].bitcast(FP8X4),
+                        rhs_scale=zs[:],
+                        start=True,
+                        stop=True,
+                    )
+                nc.scalar.copy(out=res[:, planes[0] : planes[-1] + 1, chunk(c)], in_=bank[:])
             nc.sync.dma_start(out=out_rows[:, :, chunk(c)], in_=res[:, :, chunk(c)])
 
         def round_result(cols):
@@ -215,24 +226,29 @@ def tile_picked_errfb_none_po_kernel(
                 out=o_words[:, cols].bitcast(FP8X4), scales=o_scales[:, cols], in_=rounded[:, woven_columns(cols)]
             )
 
-        chunks = S // CHUNK
-        ahead = make_z(0)
-        for c in range(chunks):
-            z_now = ahead
-            if c + 1 < chunks:
-                ahead = make_z(c + 1)
-            second_product(c, z_now)
+        one_bank = [[0, 1, 2, 3]]
+        z0 = make_z(0)
+        clip(PACK - 1, halves[1])
+        second_product(0, z0, one_bank)
+        z1 = make_z(1)
+        z2 = make_z(2)
+        second_product(1, z1, one_bank)
+        second_product(2, z2, one_bank)
+        z3 = make_z(3)
+        round_result(chunk(0))
+        second_product(3, z3, [[0, 1], [2, 3]])
+        round_result(chunk(1))
+        round_result(chunk(2))
+        hand_on(halves[0])
+        hand_on(chunk(2))
+        early = slice(0, 3 * CHUNK)
+        nc.sync.dma_start(out=out_words[:, early], in_=o_words[:, early].bitcast(I32))
+        round_result(chunk(3))
+        hand_on(chunk(3))
 
-        pieces = [halves[0], chunk(2), chunk(3)]
-        round_result(pieces[0])
-        for k, cols in enumerate(pieces):
-            if k + 1 < len(pieces):
-                round_result(pieces[k + 1])
-            hand_on(cols)
-
-        nc.sync.dma_start(out=out_words, in_=o_words[:].bitcast(I32))
+        nc.scalar.dma_start(out=out_words[:, chunk(3)], in_=o_words[:, chunk(3)].bitcast(I32))
         for q in range(4):
-            queue = nc.sync if q == 3 else nc.scalar
+            queue = nc.scalar if q % 2 else nc.sync
             queue.dma_start(
                 out=out_2[0, 4 * q : 4 * q + 4, :].bitcast(I32),
                 in_=o_scales[QUADRANT * q : QUADRANT * q + 4, :].bitcast(I32),

@@ -21,11 +21,11 @@ QUADRANT = 32
 GROUP = 16
 HALF = S // 2
 CHUNK = S // 4
+RUN = 4
 W1_ROW = 4
 W2_ROW = 8
 
-EF_BYTES = 4 * U
-W1_SCALES_AT = PACK * EF_BYTES
+GN_AT = 0
 
 
 def tile_picked_errfb_none_po_kernel(
@@ -61,10 +61,10 @@ def tile_picked_errfb_none_po_kernel(
         xs = tile([P, T], U8, "xs")
         w1w = tile([P, H], I32, "w1w")
         w2w = tile([P, N], I32, "w2w")
-        w1s = placed([P, H], U8, "w1s", W1_SCALES_AT)
+        w1s = tile([P, H], U8, "w1s")
         w2s = tile([P, N], U8, "w2s")
-        gn_t = tile([P, PACK], F32, "gn_t")
-        ef_t = [placed([P, U], F32, f"ef{t}", EF_BYTES * t) for t in range(PACK)]
+        gn_t = placed([P, PACK], F32, "gn_t", GN_AT)
+        ef_t = [tile([P, U], F32, f"ef{t}") for t in range(PACK)]
 
         nc.vector.memset(xs[:].bitcast(I32), 0)
         nc.vector.memset(w1s[:].bitcast(I32), 0)
@@ -72,12 +72,12 @@ def tile_picked_errfb_none_po_kernel(
 
         ef_rows = ef.rearrange("(p t) u -> t p u", t=PACK)
         nc.sync.dma_start(offs_t[:], offs)
-        nc.sync.dma_start(out=gn_t[:], in_=gn.rearrange("(p t) o -> p (t o)", t=PACK))
+        nc.sync.dma_start(ent_t[:], ent)
         nc.sync.dma_start(out=w1w[:], in_=words(w1_words))
         load_scale_rows(xs, 0, x_scales)
         nc.sync.dma_start(out=xw[:].bitcast(I32), in_=words(x_words))
         load_scale_rows(w1s, W1_ROW, w1_scales)
-        nc.sync.dma_start(ent_t[:], ent)
+        nc.sync.dma_start(out=gn_t[:], in_=gn.rearrange("(p t) o -> p (t o)", t=PACK))
         nc.sync.dma_start(out=w2w[:], in_=words(w2_words))
         for t in range(PACK):
             nc.sync.dma_start(out=ef_t[t][:], in_=ef_rows[t])
@@ -89,6 +89,10 @@ def tile_picked_errfb_none_po_kernel(
         nc.scalar.activation(quarter[:], gn_t[:], ACT.Copy, scale=0.25)
         nc.scalar.activation(high[:], gn_t[:], ACT.Abs, scale=0.125)
         nc.scalar.activation(low[:], high[:], ACT.Copy, scale=-1.0)
+        first = tile([P, 3], F32, "first")
+        nc.scalar.activation(first[:, 0:1], quarter[:, 0:1], ACT.Copy, scale=-1.0)
+        nc.scalar.activation(first[:, 1:2], high[:, 0:1], ACT.Copy, scale=2.0)
+        nc.scalar.activation(first[:, 2:3], high[:, 0:1], ACT.Copy, scale=-3.0)
 
         def deal_words(dst, src):
             nc.vector.tensor_copy(
@@ -108,7 +112,7 @@ def tile_picked_errfb_none_po_kernel(
         deal_words(w1d, w1w)
         xs_g = tile([P, S], U8, "xs_g")
         nc.vector.tensor_copy(xs_g[:], xs[:].indirect(offs_t[:]))
-        xw_g = [tile([P, HALF], U32, "xw_g0"), placed([P, HALF], U32, "xw_g1", W1_SCALES_AT)]
+        xw_g = [tile([P, HALF], U32, "xw_g0"), placed([P, HALF], U32, "xw_g1", GN_AT)]
         nc.vector.tensor_copy(xw_g[0][:], xw[:].indirect(list_half(offs_t, halves[0])))
         w1sd = tile([P, H], U8, "w1sd")
         deal_bytes(w1sd, w1s)
@@ -117,14 +121,17 @@ def tile_picked_errfb_none_po_kernel(
         deal_words(w2d, w2w)
 
         a = tile([P, PACK, S], F32, "a")
-        lin = tile([P, PACK, S], F32, "lin")
-        cut = tile([P, PACK, S], F32, "cut")
-        y = tile([P, PACK + 1, HALF], F32, "y")
+        lin = tile([P, PACK * S], F32, "lin")
+        cut = tile([P, PACK * S], F32, "cut")
+        y = tile([P, PACK, S], F32, "y")
+        below = tile([P, S], F32, "below")
 
-        def y_half(t, h):
-            if t > 0 and h == 0:
-                return cut[:, t - 1, halves[0]]
-            return y[:, t + h, :]
+        def runs(plane):
+            return plane.rearrange("p (c i) -> p c i", i=RUN)
+
+        def plane_of(term, t, cols):
+            view = term[:].rearrange("p (c t i) -> p t c i", t=PACK, i=RUN)
+            return view[:, t, cols.start // RUN : cols.stop // RUN, :]
 
         def first_product(out, t, h):
             nc.tensor.matmul_mx(
@@ -141,28 +148,35 @@ def tile_picked_errfb_none_po_kernel(
             for h in range(2):
                 bank = ps.tile([P, HALF], F32, name=f"y_ps{t}{h}", tag=f"bank{2 * t + h}")
                 first_product(bank[:], t, h)
-                nc.scalar.copy(out=y_half(t, h), in_=bank[:])
+                nc.scalar.copy(out=y[:, t, halves[h]], in_=bank[:])
 
         whole = slice(0, S)
 
         def clip(t, cols):
             nc.vector.tensor_scalar(
-                cut[:, t, cols], lin[:, t, cols], high[:, t : t + 1], low[:, t : t + 1], ALU.min, ALU.max
+                plane_of(cut, t, cols), plane_of(lin, t, cols), high[:, t : t + 1], low[:, t : t + 1], ALU.min, ALU.max
             )
 
         for t in range(PACK):
-            for h, cols in enumerate(halves):
+            for cols in halves:
                 nc.vector.tensor_tensor(
-                    a[:, t, cols], ef_t[t][:].indirect(list_half(ent_t, cols)), y_half(t, h), ALU.add
+                    a[:, t, cols], ef_t[t][:].indirect(list_half(ent_t, cols)), y[:, t, cols], ALU.add
                 )
+            if t == 0:
+                nc.scalar.activation(below[:], a[:, 0, :], ACT.Relu, scale=first[:, 0:1], bias=high[:, 0:1])
+                nc.scalar.activation(
+                    plane_of(lin, 0, whole), runs(a[:, 0, :]), ACT.Identity, scale=quarter[:, 0:1], bias=first[:, 2:3]
+                )
+                nc.scalar.activation(plane_of(cut, 0, whole), runs(below[:]), ACT.Relu, scale=-1.0, bias=first[:, 1:2])
+                continue
             for cols in halves if t == PACK - 1 else [whole]:
-                nc.scalar.activation(lin[:, t, cols], a[:, t, cols], ACT.Copy, scale=quarter[:, t : t + 1])
-            if t > 0:
-                clip(t - 1, whole)
+                nc.scalar.activation(plane_of(lin, t, cols), runs(a[:, t, cols]), ACT.Copy, scale=quarter[:, t : t + 1])
 
-        w2sd = placed([P, N], U8, "w2sd", EF_BYTES * (PACK - 1))
-        clip(PACK - 1, halves[0])
+        w2sd = tile([P, N], U8, "w2sd")
         deal_bytes(w2sd, w2s)
+        clip(1, whole)
+        clip(2, whole)
+        clip(PACK - 1, halves[0])
 
         o_words = tile([P, S], U32, "o_words")
         o_scales = tile([P, S], U8, "o_scales")
@@ -186,10 +200,10 @@ def tile_picked_errfb_none_po_kernel(
         def make_z(c):
             z = tile([P, PACK * CHUNK], BF16, f"z{c}")
             nc.vector.scalar_tensor_tensor(
-                z[:].rearrange("p (j t) -> p j t", t=PACK),
-                cut[:, :, chunk(c)].rearrange("p t j -> p j t"),
+                z[:].rearrange("p (i o) -> p o i", i=RUN),
+                cut[:, woven_columns(chunk(c))].rearrange("p (o i) -> p o i", i=RUN),
                 3.0,
-                lin[:, :, chunk(c)].rearrange("p t j -> p j t"),
+                lin[:, woven_columns(chunk(c))].rearrange("p (o i) -> p o i", i=RUN),
                 ALU.mult,
                 ALU.add,
             )
@@ -215,7 +229,10 @@ def tile_picked_errfb_none_po_kernel(
                         start=True,
                         stop=True,
                     )
-                nc.scalar.copy(out=res[:, planes[0] : planes[-1] + 1, chunk(c)], in_=bank[:])
+                nc.scalar.copy(
+                    out=res[:, planes[0] : planes[-1] + 1, chunk(c)].rearrange("p t (c i) -> p t c i", i=RUN),
+                    in_=bank[:].rearrange("p t (i c) -> p t c i", i=RUN),
+                )
             nc.sync.dma_start(out=out_rows[:, :, chunk(c)], in_=res[:, :, chunk(c)])
 
         def round_result(cols):

@@ -89,10 +89,12 @@ def tile_picked_errfb_none_po_kernel(
         nc.scalar.activation(quarter[:], gn_t[:], ACT.Copy, scale=0.25)
         nc.scalar.activation(high[:], gn_t[:], ACT.Abs, scale=0.125)
         nc.scalar.activation(low[:], high[:], ACT.Copy, scale=-1.0)
-        first = tile([P, 3], F32, "first")
-        nc.scalar.activation(first[:, 0:1], quarter[:, 0:1], ACT.Copy, scale=-1.0)
-        nc.scalar.activation(first[:, 1:2], high[:, 0:1], ACT.Copy, scale=2.0)
-        nc.scalar.activation(first[:, 2:3], high[:, 0:1], ACT.Copy, scale=-3.0)
+        minus_quarter = tile([P, PACK], F32, "minus_quarter")
+        twice = tile([P, PACK], F32, "twice")
+        shift = tile([P, PACK], F32, "shift")
+        nc.scalar.activation(minus_quarter[:], quarter[:], ACT.Copy, scale=-1.0)
+        nc.scalar.activation(twice[:], high[:], ACT.Copy, scale=2.0)
+        nc.scalar.activation(shift[:], high[:], ACT.Copy, scale=-3.0)
 
         def deal_words(dst, src):
             nc.vector.tensor_copy(
@@ -124,7 +126,7 @@ def tile_picked_errfb_none_po_kernel(
         lin = tile([P, PACK * S], F32, "lin")
         cut = tile([P, PACK * S], F32, "cut")
         y = tile([P, PACK, S], F32, "y")
-        below = tile([P, S], F32, "below")
+        below = tile([P, PACK, S], F32, "below")
 
         def runs(plane):
             return plane.rearrange("p (c i) -> p c i", i=RUN)
@@ -157,27 +159,40 @@ def tile_picked_errfb_none_po_kernel(
                 plane_of(cut, t, cols), plane_of(lin, t, cols), high[:, t : t + 1], low[:, t : t + 1], ALU.min, ALU.max
             )
 
-        for t in range(PACK):
+        def look_up(t):
             for cols in halves:
                 nc.vector.tensor_tensor(
                     a[:, t, cols], ef_t[t][:].indirect(list_half(ent_t, cols)), y[:, t, cols], ALU.add
                 )
-            if t == 0:
-                nc.scalar.activation(below[:], a[:, 0, :], ACT.Relu, scale=first[:, 0:1], bias=high[:, 0:1])
-                nc.scalar.activation(
-                    plane_of(lin, 0, whole), runs(a[:, 0, :]), ACT.Identity, scale=quarter[:, 0:1], bias=first[:, 2:3]
-                )
-                nc.scalar.activation(plane_of(cut, 0, whole), runs(below[:]), ACT.Relu, scale=-1.0, bias=first[:, 1:2])
-                continue
-            for cols in halves if t == PACK - 1 else [whole]:
-                nc.scalar.activation(plane_of(lin, t, cols), runs(a[:, t, cols]), ACT.Copy, scale=quarter[:, t : t + 1])
 
-        w2sd = tile([P, N], U8, "w2sd")
-        deal_bytes(w2sd, w2s)
+        def scale(t, cols):
+            nc.scalar.activation(plane_of(lin, t, cols), runs(a[:, t, cols]), ACT.Copy, scale=quarter[:, t : t + 1])
+
+        def scale_and_clip(t, cols):
+            one = slice(t, t + 1)
+            nc.scalar.activation(
+                below[:, t, cols], a[:, t, cols], ACT.Relu, scale=minus_quarter[:, one], bias=high[:, one]
+            )
+            nc.scalar.activation(
+                plane_of(lin, t, cols), runs(a[:, t, cols]), ACT.Identity, scale=quarter[:, one], bias=shift[:, one]
+            )
+            nc.scalar.activation(
+                plane_of(cut, t, cols), runs(below[:, t, cols]), ACT.Relu, scale=-1.0, bias=twice[:, one]
+            )
+
+        for t in range(PACK):
+            look_up(t)
+        scale_and_clip(0, whole)
+        scale(1, whole)
+        scale(2, whole)
+        scale(3, halves[0])
+        scale_and_clip(3, halves[1])
+
         clip(1, whole)
         clip(2, whole)
         clip(PACK - 1, halves[0])
 
+        w2sd = tile([P, N], U8, "w2sd")
         o_words = tile([P, S], U32, "o_words")
         o_scales = tile([P, S], U8, "o_scales")
         res = tile([P, PACK, S], F32, "res")
@@ -229,10 +244,13 @@ def tile_picked_errfb_none_po_kernel(
                         start=True,
                         stop=True,
                     )
-                nc.scalar.copy(
-                    out=res[:, planes[0] : planes[-1] + 1, chunk(c)].rearrange("p t (c i) -> p t c i", i=RUN),
-                    in_=bank[:].rearrange("p t (i c) -> p t c i", i=RUN),
-                )
+                in_order = res[:, planes[0] : planes[-1] + 1, chunk(c)].rearrange("p t (c i) -> p t c i", i=RUN)
+                permuted = bank[:].rearrange("p t (i c) -> p t c i", i=RUN)
+                pieces = 2 if planes[0] > 0 else 1
+                width = CHUNK // RUN // pieces
+                for k in range(pieces):
+                    part = slice(width * k, width * (k + 1))
+                    nc.scalar.copy(out=in_order[:, :, part, :], in_=permuted[:, :, part, :])
             nc.sync.dma_start(out=out_rows[:, :, chunk(c)], in_=res[:, :, chunk(c)])
 
         def round_result(cols):
@@ -245,23 +263,27 @@ def tile_picked_errfb_none_po_kernel(
 
         one_bank = [[0, 1, 2, 3]]
         z0 = make_z(0)
-        clip(PACK - 1, halves[1])
+        deal_bytes(w2sd, w2s)
         second_product(0, z0, one_bank)
+        nc.scalar.copy(out=woven_view(rounded[:, woven_columns(chunk(0))]), in_=planes_view(res[:, :, chunk(0)]))
         z1 = make_z(1)
         z2 = make_z(2)
         second_product(1, z1, one_bank)
         second_product(2, z2, one_bank)
         z3 = make_z(3)
-        round_result(chunk(0))
+        hand_on(chunk(0))
         second_product(3, z3, [[0, 1], [2, 3]])
         round_result(chunk(1))
         round_result(chunk(2))
-        hand_on(halves[0])
+        hand_on(chunk(1))
         hand_on(chunk(2))
         early = slice(0, 3 * CHUNK)
         nc.sync.dma_start(out=out_words[:, early], in_=o_words[:, early].bitcast(I32))
-        round_result(chunk(3))
-        hand_on(chunk(3))
+        ends = [slice(S - CHUNK, S - CHUNK // 2), slice(S - CHUNK // 2, S)]
+        for cols in ends:
+            round_result(cols)
+        for cols in ends:
+            hand_on(cols)
 
         nc.scalar.dma_start(out=out_words[:, chunk(3)], in_=o_words[:, chunk(3)].bitcast(I32))
         for q in range(4):

@@ -19,6 +19,9 @@ P = 128
 PACK = 4
 QUADRANT = 32
 GROUP = 16
+QUADRANTS = P // QUADRANT
+ROWS = 4
+BANKS = 8
 HALF = S // 2
 CHUNK = S // 4
 RUN = 4
@@ -26,6 +29,7 @@ W1_ROW = 4
 W2_ROW = 8
 
 GN_AT = 0
+Y_LAST_AT = 4 * HALF
 
 
 def tile_picked_errfb_none_po_kernel(
@@ -47,13 +51,15 @@ def tile_picked_errfb_none_po_kernel(
             return dram[0].rearrange("p n t -> p (n t)").bitcast(I32)
 
         def load_scale_rows(scale_tile, first, dram):
-            for q in range(4):
+            for q in range(QUADRANTS):
                 nc.sync.dma_start(
-                    out=scale_tile[QUADRANT * q + first : QUADRANT * q + first + 4, :].bitcast(I32),
-                    in_=dram[0, 4 * q : 4 * q + 4, :].bitcast(I32),
+                    out=scale_tile[QUADRANT * q + first : QUADRANT * q + first + ROWS, :].bitcast(I32),
+                    in_=dram[0, ROWS * q : ROWS * (q + 1), :].bitcast(I32),
                 )
 
+        whole = slice(0, S)
         halves = [slice(0, HALF), slice(HALF, S)]
+        last_plane = PACK - 1
 
         offs_t = tile([P, S // GROUP], U16, "offs_t")
         ent_t = tile([P, S // GROUP], U16, "ent_t")
@@ -85,21 +91,13 @@ def tile_picked_errfb_none_po_kernel(
 
         quarter = tile([P, PACK], F32, "quarter")
         high = tile([P, PACK], F32, "high")
-        low = tile([P, PACK], F32, "low")
         nc.scalar.activation(quarter[:], gn_t[:], ACT.Copy, scale=0.25)
         nc.scalar.activation(high[:], gn_t[:], ACT.Abs, scale=0.125)
-        nc.scalar.activation(low[:], high[:], ACT.Copy, scale=-1.0)
-        minus_quarter = tile([P, PACK], F32, "minus_quarter")
-        twice = tile([P, PACK], F32, "twice")
-        shift = tile([P, PACK], F32, "shift")
-        nc.scalar.activation(minus_quarter[:], quarter[:], ACT.Copy, scale=-1.0)
-        nc.scalar.activation(twice[:], high[:], ACT.Copy, scale=2.0)
-        nc.scalar.activation(shift[:], high[:], ACT.Copy, scale=-3.0)
 
         def deal_words(dst, src):
             nc.vector.tensor_copy(
-                out=dst[:].rearrange("p (u e c i) -> p c u i e", u=2, e=2, i=4),
-                in_=src[:].rearrange("p (c i u e) -> p c u i e", u=2, e=2, i=4),
+                out=dst[:].rearrange("p (u e r i) -> p r u i e", u=2, e=2, i=4),
+                in_=src[:].rearrange("p (r i u e) -> p r u i e", u=2, e=2, i=4),
             )
 
         def deal_bytes(dst, src):
@@ -107,7 +105,7 @@ def tile_picked_errfb_none_po_kernel(
                 out=dst[:].rearrange("p (t m) -> p t m", t=PACK), in_=src[:].rearrange("p (m t) -> p t m", t=PACK)
             )
 
-        def list_half(list_tile, cols):
+        def entries(list_tile, cols):
             return list_tile[:, cols.start // GROUP : cols.stop // GROUP]
 
         w1d = tile([P, H], I32, "w1d")
@@ -115,10 +113,10 @@ def tile_picked_errfb_none_po_kernel(
         xs_g = tile([P, S], U8, "xs_g")
         nc.vector.tensor_copy(xs_g[:], xs[:].indirect(offs_t[:]))
         xw_g = [tile([P, HALF], U32, "xw_g0"), placed([P, HALF], U32, "xw_g1", GN_AT)]
-        nc.vector.tensor_copy(xw_g[0][:], xw[:].indirect(list_half(offs_t, halves[0])))
+        nc.vector.tensor_copy(xw_g[0][:], xw[:].indirect(entries(offs_t, halves[0])))
         w1sd = tile([P, H], U8, "w1sd")
         deal_bytes(w1sd, w1s)
-        nc.vector.tensor_copy(xw_g[1][:], xw[:].indirect(list_half(offs_t, halves[1])))
+        nc.vector.tensor_copy(xw_g[1][:], xw[:].indirect(entries(offs_t, halves[1])))
         w2d = tile([P, N], I32, "w2d")
         deal_words(w2d, w2w)
 
@@ -126,71 +124,63 @@ def tile_picked_errfb_none_po_kernel(
         lin = tile([P, PACK * S], F32, "lin")
         cut = tile([P, PACK * S], F32, "cut")
         y = tile([P, PACK, S], F32, "y")
-        below = tile([P, PACK, S], F32, "below")
+        y_last = placed([P, HALF], F32, "y_last", Y_LAST_AT)
+
+        def y_part(t, cols):
+            return y_last[:] if (t, cols) == (last_plane, halves[0]) else y[:, t, cols]
 
         def runs(plane):
-            return plane.rearrange("p (c i) -> p c i", i=RUN)
+            return plane.rearrange("p (r i) -> p r i", i=RUN)
 
         def plane_of(term, t, cols):
-            view = term[:].rearrange("p (c t i) -> p t c i", t=PACK, i=RUN)
+            view = term[:].rearrange("p (r t i) -> p t r i", t=PACK, i=RUN)
             return view[:, t, cols.start // RUN : cols.stop // RUN, :]
 
-        def first_product(out, t, h):
+        def first_product(t, h, part, b):
+            cols = slice(HALF * h + part.start, HALF * h + part.stop)
+            bank = ps.tile([P, part.stop - part.start], F32, name=f"y_ps{t}{cols.start}", tag=f"bank{b}")
             nc.tensor.matmul_mx(
-                out=out,
+                out=bank[:],
                 lhsT=w1d[:, P * t : P * (t + 1)].bitcast(FP8X4),
                 lhsT_scale=w1sd[W1_ROW:P, P * t : P * (t + 1)],
-                rhs=xw_g[h][:].bitcast(FP8X4),
-                rhs_scale=xs_g[:, halves[h]],
+                rhs=xw_g[h][:, part].bitcast(FP8X4),
+                rhs_scale=xs_g[:, cols],
                 start=True,
                 stop=True,
             )
+            nc.scalar.copy(out=y_part(t, cols), in_=bank[:])
 
-        for t in range(PACK):
-            for h in range(2):
-                bank = ps.tile([P, HALF], F32, name=f"y_ps{t}{h}", tag=f"bank{2 * t + h}")
-                first_product(bank[:], t, h)
-                nc.scalar.copy(out=y[:, t, halves[h]], in_=bank[:])
-
-        whole = slice(0, S)
+        first_product(0, 0, slice(0, CHUNK), BANKS - 1)
+        first_product(0, 0, slice(CHUNK, HALF), 0)
+        for b in range(1, BANKS):
+            first_product(b // 2, b % 2, slice(0, HALF), b)
 
         def clip(t, cols):
             nc.vector.tensor_scalar(
                 plane_of(cut, t, cols), plane_of(lin, t, cols), high[:, t : t + 1], low[:, t : t + 1], ALU.min, ALU.max
             )
 
-        def look_up(t):
-            for cols in halves:
-                nc.vector.tensor_tensor(
-                    a[:, t, cols], ef_t[t][:].indirect(list_half(ent_t, cols)), y[:, t, cols], ALU.add
-                )
+        def look_up(t, cols):
+            nc.vector.tensor_tensor(a[:, t, cols], ef_t[t][:].indirect(entries(ent_t, cols)), y_part(t, cols), ALU.add)
 
         def scale(t, cols):
             nc.scalar.activation(plane_of(lin, t, cols), runs(a[:, t, cols]), ACT.Copy, scale=quarter[:, t : t + 1])
 
-        def scale_and_clip(t, cols):
-            one = slice(t, t + 1)
-            nc.scalar.activation(
-                below[:, t, cols], a[:, t, cols], ACT.Relu, scale=minus_quarter[:, one], bias=high[:, one]
-            )
-            nc.scalar.activation(
-                plane_of(lin, t, cols), runs(a[:, t, cols]), ACT.Identity, scale=quarter[:, one], bias=shift[:, one]
-            )
-            nc.scalar.activation(
-                plane_of(cut, t, cols), runs(below[:, t, cols]), ACT.Relu, scale=-1.0, bias=twice[:, one]
-            )
-
         for t in range(PACK):
-            look_up(t)
-        scale_and_clip(0, whole)
-        scale(1, whole)
-        scale(2, whole)
-        scale(3, halves[0])
-        scale_and_clip(3, halves[1])
+            for cols in [whole] if t == 2 else halves:
+                look_up(t, cols)
+        for t in range(last_plane):
+            scale(t, whole)
+        low = placed([P, PACK], F32, "low", Y_LAST_AT)
+        nc.scalar.activation(low[:], high[:], ACT.Copy, scale=-1.0)
+        for cols in halves:
+            scale(last_plane, cols)
 
+        clip(0, whole)
         clip(1, whole)
-        clip(2, whole)
-        clip(PACK - 1, halves[0])
+        clip(2, halves[0])
+        clip(last_plane, halves[0])
+        clip(2, halves[1])
 
         w2sd = tile([P, N], U8, "w2sd")
         o_words = tile([P, S], U32, "o_words")
@@ -201,10 +191,10 @@ def tile_picked_errfb_none_po_kernel(
         out_words = words(out_1)
 
         def woven_view(woven):
-            return woven.rearrange("p (c i t) -> p c t i", t=PACK, i=2)
+            return woven.rearrange("p (r i t) -> p r t i", t=PACK, i=RUN)
 
         def planes_view(planes):
-            return planes.rearrange("p t (c i) -> p c t i", i=2)
+            return planes.rearrange("p t (r i) -> p r t i", i=RUN)
 
         def chunk(c):
             return slice(CHUNK * c, CHUNK * (c + 1))
@@ -224,14 +214,11 @@ def tile_picked_errfb_none_po_kernel(
             )
             return z
 
-        def quantise_z(c, z):
+        def second_product(c, z, last=False):
             zw = tile([P, CHUNK], U32, f"zw{c}")
             zs = tile([P, CHUNK], U8, f"zs{c}")
             nc.vector.quantize_mx(out=zw[:].bitcast(FP8X4), scales=zs[:], in_=z[:])
-            return zw, zs
-
-        def second_product(c, z, groups):
-            zw, zs = quantise_z(c, z)
+            groups = [range(0, 2), range(2, PACK)] if last else [range(PACK)]
             for g, planes in enumerate(groups):
                 bank = ps.tile([P, len(planes), CHUNK], F32, name=f"o_ps{c}{g}", tag=f"bank{c + g}")
                 for k, t in enumerate(planes):
@@ -244,9 +231,9 @@ def tile_picked_errfb_none_po_kernel(
                         start=True,
                         stop=True,
                     )
-                in_order = res[:, planes[0] : planes[-1] + 1, chunk(c)].rearrange("p t (c i) -> p t c i", i=RUN)
-                permuted = bank[:].rearrange("p t (i c) -> p t c i", i=RUN)
-                pieces = 2 if planes[0] > 0 else 1
+                in_order = res[:, planes.start : planes.stop, chunk(c)].rearrange("p t (r i) -> p t r i", i=RUN)
+                permuted = bank[:].rearrange("p t (i r) -> p t r i", i=RUN)
+                pieces = 2 if g == 1 else 1
                 width = CHUNK // RUN // pieces
                 for k in range(pieces):
                     part = slice(width * k, width * (k + 1))
@@ -261,23 +248,23 @@ def tile_picked_errfb_none_po_kernel(
                 out=o_words[:, cols].bitcast(FP8X4), scales=o_scales[:, cols], in_=rounded[:, woven_columns(cols)]
             )
 
-        one_bank = [[0, 1, 2, 3]]
         z0 = make_z(0)
         deal_bytes(w2sd, w2s)
-        second_product(0, z0, one_bank)
+        second_product(0, z0)
         nc.scalar.copy(out=woven_view(rounded[:, woven_columns(chunk(0))]), in_=planes_view(res[:, :, chunk(0)]))
         z1 = make_z(1)
+        clip(last_plane, halves[1])
+        second_product(1, z1)
         z2 = make_z(2)
-        second_product(1, z1, one_bank)
-        second_product(2, z2, one_bank)
-        z3 = make_z(3)
         hand_on(chunk(0))
-        second_product(3, z3, [[0, 1], [2, 3]])
+        second_product(2, z2)
+        z3 = make_z(3)
         round_result(chunk(1))
+        second_product(3, z3, last=True)
         round_result(chunk(2))
         hand_on(chunk(1))
         hand_on(chunk(2))
-        early = slice(0, 3 * CHUNK)
+        early = slice(0, chunk(3).start)
         nc.sync.dma_start(out=out_words[:, early], in_=o_words[:, early].bitcast(I32))
         ends = [slice(S - CHUNK, S - CHUNK // 2), slice(S - CHUNK // 2, S)]
         for cols in ends:
@@ -286,9 +273,9 @@ def tile_picked_errfb_none_po_kernel(
             hand_on(cols)
 
         nc.scalar.dma_start(out=out_words[:, chunk(3)], in_=o_words[:, chunk(3)].bitcast(I32))
-        for q in range(4):
+        for q in range(QUADRANTS):
             queue = nc.scalar if q % 2 else nc.sync
             queue.dma_start(
-                out=out_2[0, 4 * q : 4 * q + 4, :].bitcast(I32),
-                in_=o_scales[QUADRANT * q : QUADRANT * q + 4, :].bitcast(I32),
+                out=out_2[0, ROWS * q : ROWS * (q + 1), :].bitcast(I32),
+                in_=o_scales[QUADRANT * q : QUADRANT * q + ROWS, :].bitcast(I32),
             )

@@ -21,7 +21,6 @@ QUADRANT = 32
 GROUP = 16
 QUADRANTS = P // QUADRANT
 ROWS = 4
-BANKS = 8
 HALF = S // 2
 CHUNK = S // 4
 RUN = 4
@@ -29,7 +28,7 @@ W1_ROW = 4
 W2_ROW = 8
 
 GN_AT = 0
-Y_LAST_AT = 4 * HALF
+Y_LAST_AT = GN_AT + 4 * HALF
 
 
 def tile_picked_errfb_none_po_kernel(
@@ -136,24 +135,19 @@ def tile_picked_errfb_none_po_kernel(
             view = term[:].rearrange("p (r t i) -> p t r i", t=PACK, i=RUN)
             return view[:, t, cols.start // RUN : cols.stop // RUN, :]
 
-        def first_product(t, h, part, b):
-            cols = slice(HALF * h + part.start, HALF * h + part.stop)
-            bank = ps.tile([P, part.stop - part.start], F32, name=f"y_ps{t}{cols.start}", tag=f"bank{b}")
-            nc.tensor.matmul_mx(
-                out=bank[:],
-                lhsT=w1d[:, P * t : P * (t + 1)].bitcast(FP8X4),
-                lhsT_scale=w1sd[W1_ROW:P, P * t : P * (t + 1)],
-                rhs=xw_g[h][:, part].bitcast(FP8X4),
-                rhs_scale=xs_g[:, cols],
-                start=True,
-                stop=True,
-            )
-            nc.scalar.copy(out=y_part(t, cols), in_=bank[:])
-
-        first_product(0, 0, slice(0, CHUNK), BANKS - 1)
-        first_product(0, 0, slice(CHUNK, HALF), 0)
-        for b in range(1, BANKS):
-            first_product(b // 2, b % 2, slice(0, HALF), b)
+        for t in range(PACK):
+            for h, cols in enumerate(halves):
+                bank = ps.tile([P, HALF], F32, name=f"y_ps{t}{h}", tag=f"bank{2 * t + h}")
+                nc.tensor.matmul_mx(
+                    out=bank[:],
+                    lhsT=w1d[:, P * t : P * (t + 1)].bitcast(FP8X4),
+                    lhsT_scale=w1sd[W1_ROW:P, P * t : P * (t + 1)],
+                    rhs=xw_g[h][:].bitcast(FP8X4),
+                    rhs_scale=xs_g[:, cols],
+                    start=True,
+                    stop=True,
+                )
+                nc.scalar.copy(out=y_part(t, cols), in_=bank[:])
 
         def clip(t, cols):
             nc.vector.tensor_scalar(
@@ -191,10 +185,10 @@ def tile_picked_errfb_none_po_kernel(
         out_words = words(out_1)
 
         def woven_view(woven):
-            return woven.rearrange("p (r i t) -> p r t i", t=PACK, i=RUN)
+            return woven.rearrange("p (r i t) -> p r t i", t=PACK, i=2)
 
         def planes_view(planes):
-            return planes.rearrange("p t (r i) -> p r t i", i=RUN)
+            return planes.rearrange("p t (r i) -> p r t i", i=2)
 
         def chunk(c):
             return slice(CHUNK * c, CHUNK * (c + 1))
@@ -218,9 +212,9 @@ def tile_picked_errfb_none_po_kernel(
             zw = tile([P, CHUNK], U32, f"zw{c}")
             zs = tile([P, CHUNK], U8, f"zs{c}")
             nc.vector.quantize_mx(out=zw[:].bitcast(FP8X4), scales=zs[:], in_=z[:])
-            groups = [range(0, 2), range(2, PACK)] if last else [range(PACK)]
-            for g, planes in enumerate(groups):
-                bank = ps.tile([P, len(planes), CHUNK], F32, name=f"o_ps{c}{g}", tag=f"bank{c + g}")
+            bank_planes = [range(0, 2), range(2, PACK)] if last else [range(PACK)]
+            for pair, planes in enumerate(bank_planes):
+                bank = ps.tile([P, len(planes), CHUNK], F32, name=f"o_ps{c}{pair}", tag=f"bank{c + pair}")
                 for k, t in enumerate(planes):
                     nc.tensor.matmul_mx(
                         out=bank[:, k, :],
@@ -233,7 +227,7 @@ def tile_picked_errfb_none_po_kernel(
                     )
                 in_order = res[:, planes.start : planes.stop, chunk(c)].rearrange("p t (r i) -> p t r i", i=RUN)
                 permuted = bank[:].rearrange("p t (i r) -> p t r i", i=RUN)
-                pieces = 2 if g == 1 else 1
+                pieces = 2 if pair == 1 else 1
                 width = CHUNK // RUN // pieces
                 for k in range(pieces):
                     part = slice(width * k, width * (k + 1))

@@ -27,9 +27,6 @@ RUN = 4
 W1_ROW = 4
 W2_ROW = 8
 
-GN_AT = 0
-Y_LAST_AT = GN_AT + 4 * HALF
-
 
 def tile_picked_errfb_none_po_kernel(
     tc, x_words, x_scales, w1_words, w1_scales, ef, gn, w2_words, w2_scales, offs, ent, out_0, out_1, out_2
@@ -43,20 +40,19 @@ def tile_picked_errfb_none_po_kernel(
         def tile(shape, dtype, name):
             return sb.tile(shape, dtype, name=name, align_bytes=64)
 
-        def placed(shape, dtype, name, offset):
+        def placed(shape, dtype, name, offset=0):
             return shared.tile(shape, dtype, name=name, align_bytes=64, offset=offset)
 
         def words(dram):
             return dram[0].rearrange("p n t -> p (n t)").bitcast(I32)
 
         def load_scale_rows(scale_tile, first, dram):
-            for q in range(QUADRANTS):
+            for r in range(ROWS):
                 nc.sync.dma_start(
-                    out=scale_tile[QUADRANT * q + first : QUADRANT * q + first + ROWS, :].bitcast(I32),
-                    in_=dram[0, ROWS * q : ROWS * (q + 1), :].bitcast(I32),
+                    out=scale_tile[first + r : P : QUADRANT, :].bitcast(I32),
+                    in_=dram[0, r : ROWS * QUADRANTS : ROWS, :].bitcast(I32),
                 )
 
-        whole = slice(0, S)
         halves = [slice(0, HALF), slice(HALF, S)]
         last_plane = PACK - 1
 
@@ -68,7 +64,7 @@ def tile_picked_errfb_none_po_kernel(
         w2w = tile([P, N], I32, "w2w")
         w1s = tile([P, H], U8, "w1s")
         w2s = tile([P, N], U8, "w2s")
-        gn_t = placed([P, PACK], F32, "gn_t", GN_AT)
+        gn_t = placed([P, PACK], F32, "gn_t")
         ef_t = [tile([P, U], F32, f"ef{t}") for t in range(PACK)]
 
         nc.vector.memset(xs[:].bitcast(I32), 0)
@@ -83,15 +79,18 @@ def tile_picked_errfb_none_po_kernel(
         nc.sync.dma_start(out=xw[:].bitcast(I32), in_=words(x_words))
         load_scale_rows(w1s, W1_ROW, w1_scales)
         nc.sync.dma_start(out=gn_t[:], in_=gn.rearrange("(p t) o -> p (t o)", t=PACK))
-        nc.sync.dma_start(out=w2w[:], in_=words(w2_words))
-        for t in range(PACK):
+        for t in range(last_plane):
             nc.sync.dma_start(out=ef_t[t][:], in_=ef_rows[t])
         load_scale_rows(w2s, W2_ROW, w2_scales)
+        nc.sync.dma_start(out=ef_t[last_plane][:], in_=ef_rows[last_plane])
+        nc.sync.dma_start(out=w2w[:], in_=words(w2_words))
 
         quarter = tile([P, PACK], F32, "quarter")
         high = tile([P, PACK], F32, "high")
         nc.scalar.activation(quarter[:], gn_t[:], ACT.Copy, scale=0.25)
+        low = tile([P, PACK], F32, "low")
         nc.scalar.activation(high[:], gn_t[:], ACT.Abs, scale=0.125)
+        nc.scalar.activation(low[:], high[:], ACT.Copy, scale=-1.0)
 
         def deal_words(dst, src):
             nc.vector.tensor_copy(
@@ -111,22 +110,16 @@ def tile_picked_errfb_none_po_kernel(
         deal_words(w1d, w1w)
         xs_g = tile([P, S], U8, "xs_g")
         nc.vector.tensor_copy(xs_g[:], xs[:].indirect(offs_t[:]))
-        xw_g = [tile([P, HALF], U32, "xw_g0"), placed([P, HALF], U32, "xw_g1", GN_AT)]
-        nc.vector.tensor_copy(xw_g[0][:], xw[:].indirect(entries(offs_t, halves[0])))
         w1sd = tile([P, H], U8, "w1sd")
+        xw_g = [tile([P, HALF], U32, "xw_g0"), placed([P, HALF], U32, "xw_g1")]
+        nc.vector.tensor_copy(xw_g[0][:], xw[:].indirect(entries(offs_t, halves[0])))
         deal_bytes(w1sd, w1s)
         nc.vector.tensor_copy(xw_g[1][:], xw[:].indirect(entries(offs_t, halves[1])))
-        w2d = tile([P, N], I32, "w2d")
-        deal_words(w2d, w2w)
 
-        a = tile([P, PACK, S], F32, "a")
+        looked = [tile([P, S], F32, f"looked{t}") for t in range(PACK)]
+        scaled = [tile([P, S], F32, f"scaled{t}") for t in range(PACK)]
         lin = tile([P, PACK * S], F32, "lin")
         cut = tile([P, PACK * S], F32, "cut")
-        y = tile([P, PACK, S], F32, "y")
-        y_last = placed([P, HALF], F32, "y_last", Y_LAST_AT)
-
-        def y_part(t, cols):
-            return y_last[:] if (t, cols) == (last_plane, halves[0]) else y[:, t, cols]
 
         def runs(plane):
             return plane.rearrange("p (r i) -> p r i", i=RUN)
@@ -135,11 +128,16 @@ def tile_picked_errfb_none_po_kernel(
             view = term[:].rearrange("p (r t i) -> p t r i", t=PACK, i=RUN)
             return view[:, t, cols.start // RUN : cols.stop // RUN, :]
 
+        y = [ps.tile([P, S], F32, name=f"y_ps{t}", tag=f"bank{t}") for t in range(PACK)]
+        y_first = ps.tile([P, HALF], F32, name="y_first", tag="bank4")
+
+        def y_part(t, cols):
+            return y_first[:] if (t, cols) == (0, halves[0]) else y[t][:, cols]
+
         for t in range(PACK):
             for h, cols in enumerate(halves):
-                bank = ps.tile([P, HALF], F32, name=f"y_ps{t}{h}", tag=f"bank{2 * t + h}")
                 nc.tensor.matmul_mx(
-                    out=bank[:],
+                    out=y_part(t, cols),
                     lhsT=w1d[:, P * t : P * (t + 1)].bitcast(FP8X4),
                     lhsT_scale=w1sd[W1_ROW:P, P * t : P * (t + 1)],
                     rhs=xw_g[h][:].bitcast(FP8X4),
@@ -147,36 +145,54 @@ def tile_picked_errfb_none_po_kernel(
                     start=True,
                     stop=True,
                 )
-                nc.scalar.copy(out=y_part(t, cols), in_=bank[:])
+
+        def look_up(t, cols):
+            window = ef_t[t][:].indirect(entries(ent_t, cols))
+            if (t, cols) == (0, halves[1]):
+                nc.vector.tensor_copy(looked[t][:, cols], window)
+            else:
+                nc.scalar.activation(looked[t][:, cols], window, ACT.Copy)
+
+        def scale(t, cols):
+            nc.gpsimd.tensor_scalar(scaled[t][:, cols], looked[t][:, cols], quarter[:, t : t + 1], 0.0, ALU.mult, ALU.add)
+
+        def add(t, cols):
+            nc.vector.scalar_tensor_tensor(
+                plane_of(lin, t, cols),
+                runs(y_part(t, cols)),
+                quarter[:, t : t + 1],
+                runs(scaled[t][:, cols]),
+                ALU.mult,
+                ALU.add,
+            )
 
         def clip(t, cols):
             nc.vector.tensor_scalar(
                 plane_of(cut, t, cols), plane_of(lin, t, cols), high[:, t : t + 1], low[:, t : t + 1], ALU.min, ALU.max
             )
 
-        def look_up(t, cols):
-            nc.vector.tensor_tensor(a[:, t, cols], ef_t[t][:].indirect(entries(ent_t, cols)), y_part(t, cols), ALU.add)
-
-        def scale(t, cols):
-            nc.scalar.activation(plane_of(lin, t, cols), runs(a[:, t, cols]), ACT.Copy, scale=quarter[:, t : t + 1])
-
         for t in range(PACK):
-            for cols in [whole] if t == 2 else halves:
+            for cols in halves:
                 look_up(t, cols)
-        for t in range(last_plane):
-            scale(t, whole)
-        low = placed([P, PACK], F32, "low", Y_LAST_AT)
-        nc.scalar.activation(low[:], high[:], ACT.Copy, scale=-1.0)
-        for cols in halves:
-            scale(last_plane, cols)
-
-        clip(0, whole)
-        clip(1, whole)
-        clip(2, halves[0])
-        clip(last_plane, halves[0])
-        clip(2, halves[1])
-
+                scale(t, cols)
+        w2d = tile([P, N], U32, "w2d")
+        nc.scalar.copy(
+            out=w2d[:].rearrange("p (u e r i) -> p r u i e", u=2, e=2, i=4),
+            in_=w2w[:].bitcast(U32).rearrange("p (r i u e) -> p r u i e", u=2, e=2, i=4),
+        )
+        whole = slice(0, S)
         w2sd = tile([P, N], U8, "w2sd")
+        for t in range(last_plane):
+            add(t, halves[0])
+            if t > 0:
+                clip(t - 1, whole)
+            add(t, halves[1])
+        deal_bytes(w2sd, w2s)
+        add(3, halves[0])
+        clip(2, whole)
+        clip(3, halves[0])
+        add(3, halves[1])
+
         o_words = tile([P, S], U32, "o_words")
         o_scales = tile([P, S], U8, "o_scales")
         res = tile([P, PACK, S], F32, "res")
@@ -214,7 +230,7 @@ def tile_picked_errfb_none_po_kernel(
             nc.vector.quantize_mx(out=zw[:].bitcast(FP8X4), scales=zs[:], in_=z[:])
             bank_planes = [range(0, 2), range(2, PACK)] if last else [range(PACK)]
             for pair, planes in enumerate(bank_planes):
-                bank = ps.tile([P, len(planes), CHUNK], F32, name=f"o_ps{c}{pair}", tag=f"bank{c + pair}")
+                bank = ps.tile([P, len(planes), CHUNK], F32, name=f"o_ps{c}{pair}", tag=f"bank{(5 + c + pair) % 8}")
                 for k, t in enumerate(planes):
                     nc.tensor.matmul_mx(
                         out=bank[:, k, :],
@@ -243,18 +259,17 @@ def tile_picked_errfb_none_po_kernel(
             )
 
         z0 = make_z(0)
-        deal_bytes(w2sd, w2s)
+        clip(last_plane, halves[1])
         second_product(0, z0)
         nc.scalar.copy(out=woven_view(rounded[:, woven_columns(chunk(0))]), in_=planes_view(res[:, :, chunk(0)]))
         z1 = make_z(1)
-        clip(last_plane, halves[1])
-        second_product(1, z1)
         z2 = make_z(2)
-        hand_on(chunk(0))
-        second_product(2, z2)
+        second_product(1, z1)
         z3 = make_z(3)
-        round_result(chunk(1))
+        second_product(2, z2)
         second_product(3, z3, last=True)
+        round_result(chunk(1))
+        hand_on(chunk(0))
         round_result(chunk(2))
         hand_on(chunk(1))
         hand_on(chunk(2))

@@ -23,6 +23,7 @@ QUADRANTS = P // QUADRANT
 ROWS = 4
 HALF = S // 2
 CHUNK = S // 4
+Z_AT = 4 * HALF
 RUN = 4
 W1_ROW = 4
 W2_ROW = 8
@@ -79,10 +80,9 @@ def tile_picked_errfb_none_po_kernel(
         nc.sync.dma_start(out=xw[:].bitcast(I32), in_=words(x_words))
         load_scale_rows(w1s, W1_ROW, w1_scales)
         nc.sync.dma_start(out=gn_t[:], in_=gn.rearrange("(p t) o -> p (t o)", t=PACK))
-        for t in range(last_plane):
+        for t in range(PACK):
             nc.sync.dma_start(out=ef_t[t][:], in_=ef_rows[t])
         load_scale_rows(w2s, W2_ROW, w2_scales)
-        nc.sync.dma_start(out=ef_t[last_plane][:], in_=ef_rows[last_plane])
         nc.sync.dma_start(out=w2w[:], in_=words(w2_words))
 
         quarter = tile([P, PACK], F32, "quarter")
@@ -174,7 +174,8 @@ def tile_picked_errfb_none_po_kernel(
         for t in range(PACK):
             for cols in halves:
                 look_up(t, cols)
-                scale(t, cols)
+                if (t, cols) != (last_plane, halves[0]):
+                    scale(t, cols)
         w2d = tile([P, N], U32, "w2d")
         nc.scalar.copy(
             out=w2d[:].rearrange("p (u e r i) -> p r u i e", u=2, e=2, i=4),
@@ -187,16 +188,19 @@ def tile_picked_errfb_none_po_kernel(
             if t > 0:
                 clip(t - 1, whole)
             add(t, halves[1])
-        deal_bytes(w2sd, w2s)
-        add(3, halves[0])
+        a_last = scaled[last_plane][:, halves[0]]
+        nc.vector.tensor_tensor(a_last, y_part(last_plane, halves[0]), looked[last_plane][:, halves[0]], ALU.add)
         clip(2, whole)
+        nc.vector.tensor_scalar(
+            plane_of(lin, last_plane, halves[0]), runs(a_last), quarter[:, last_plane:PACK], None, ALU.mult
+        )
+        deal_bytes(w2sd, w2s)
         clip(3, halves[0])
-        add(3, halves[1])
 
         o_words = tile([P, S], U32, "o_words")
         o_scales = tile([P, S], U8, "o_scales")
-        res = tile([P, PACK, S], F32, "res")
-        rounded = tile([P, PACK * S], BF16, "rounded")
+        res = tile([P, S // CHUNK, PACK, CHUNK], F32, "res")
+        rounded = {}
         out_rows = out_0.rearrange("(p t) j -> p t j", t=PACK)
         out_words = words(out_1)
 
@@ -213,7 +217,7 @@ def tile_picked_errfb_none_po_kernel(
             return slice(PACK * cols.start, PACK * cols.stop)
 
         def make_z(c):
-            z = tile([P, PACK * CHUNK], BF16, f"z{c}")
+            z = placed([P, PACK * CHUNK], BF16, "z2", Z_AT) if c == 2 else tile([P, PACK * CHUNK], BF16, f"z{c}")
             nc.vector.scalar_tensor_tensor(
                 z[:].rearrange("p (i o) -> p o i", i=RUN),
                 cut[:, woven_columns(chunk(c))].rearrange("p (o i) -> p o i", i=RUN),
@@ -228,58 +232,54 @@ def tile_picked_errfb_none_po_kernel(
             zw = tile([P, CHUNK], U32, f"zw{c}")
             zs = tile([P, CHUNK], U8, f"zs{c}")
             nc.vector.quantize_mx(out=zw[:].bitcast(FP8X4), scales=zs[:], in_=z[:])
-            bank_planes = [range(0, 2), range(2, PACK)] if last else [range(PACK)]
-            for pair, planes in enumerate(bank_planes):
-                bank = ps.tile([P, len(planes), CHUNK], F32, name=f"o_ps{c}{pair}", tag=f"bank{(5 + c + pair) % 8}")
-                for k, t in enumerate(planes):
-                    nc.tensor.matmul_mx(
-                        out=bank[:, k, :],
-                        lhsT=w2d[:, P * t : P * (t + 1)].bitcast(FP8X4),
-                        lhsT_scale=w2sd[W2_ROW:P, P * t : P * (t + 1)],
-                        rhs=zw[:].bitcast(FP8X4),
-                        rhs_scale=zs[:],
-                        start=True,
-                        stop=True,
-                    )
-                in_order = res[:, planes.start : planes.stop, chunk(c)].rearrange("p t (r i) -> p t r i", i=RUN)
-                permuted = bank[:].rearrange("p t (i r) -> p t r i", i=RUN)
-                pieces = 2 if pair == 1 else 1
-                width = CHUNK // RUN // pieces
-                for k in range(pieces):
-                    part = slice(width * k, width * (k + 1))
-                    nc.scalar.copy(out=in_order[:, :, part, :], in_=permuted[:, :, part, :])
-            nc.sync.dma_start(out=out_rows[:, :, chunk(c)], in_=res[:, :, chunk(c)])
-
-        def round_result(cols):
-            nc.vector.tensor_copy(out=woven_view(rounded[:, woven_columns(cols)]), in_=planes_view(res[:, :, cols]))
-
-        def hand_on(cols):
-            nc.vector.quantize_mx(
-                out=o_words[:, cols].bitcast(FP8X4), scales=o_scales[:, cols], in_=rounded[:, woven_columns(cols)]
+            bank = ps.tile([P, PACK, CHUNK], F32, name=f"o_ps{c}", tag=f"bank{(5 + c) % 8}")
+            for t in range(PACK):
+                nc.tensor.matmul_mx(
+                    out=bank[:, t, :],
+                    lhsT=w2d[:, P * t : P * (t + 1)].bitcast(FP8X4),
+                    lhsT_scale=w2sd[W2_ROW:P, P * t : P * (t + 1)],
+                    rhs=zw[:].bitcast(FP8X4),
+                    rhs_scale=zs[:],
+                    start=True,
+                    stop=True,
+                )
+            nc.scalar.copy(
+                out=res[:, c].rearrange("p t (r i) -> p t r i", i=RUN),
+                in_=bank[:].rearrange("p t (i r) -> p t r i", i=RUN),
             )
+            if last:
+                nc.scalar.copy(
+                    out=rounded[c].rearrange("p (r i t) -> p r i t", i=RUN, t=PACK),
+                    in_=bank[:].rearrange("p t (i r) -> p r i t", i=RUN),
+                )
+            nc.sync.dma_start(out=out_rows[:, :, chunk(c)], in_=res[:, c])
+
+        def round_result(c):
+            nc.vector.tensor_copy(out=woven_view(rounded[c]), in_=planes_view(res[:, c]))
+
+        def hand_on(cols, woven):
+            nc.vector.quantize_mx(out=o_words[:, cols].bitcast(FP8X4), scales=o_scales[:, cols], in_=woven)
+
+        rounded[3] = tile([P, PACK * CHUNK], BF16, "rounded3")[:]
 
         z0 = make_z(0)
-        clip(last_plane, halves[1])
+        add(3, halves[1])
         second_product(0, z0)
-        nc.scalar.copy(out=woven_view(rounded[:, woven_columns(chunk(0))]), in_=planes_view(res[:, :, chunk(0)]))
         z1 = make_z(1)
-        z2 = make_z(2)
+        clip(last_plane, halves[1])
         second_product(1, z1)
+        z2 = make_z(2)
         z3 = make_z(3)
         second_product(2, z2)
         second_product(3, z3, last=True)
-        round_result(chunk(1))
-        hand_on(chunk(0))
-        round_result(chunk(2))
-        hand_on(chunk(1))
-        hand_on(chunk(2))
-        early = slice(0, chunk(3).start)
+        first_three = placed([P, 3 * PACK * CHUNK], BF16, "rounded012", Z_AT)
+        for c in range(3):
+            rounded[c] = first_three[:, woven_columns(chunk(c))]
+            round_result(c)
+        early = slice(0, 3 * CHUNK)
+        hand_on(early, first_three[:])
         nc.sync.dma_start(out=out_words[:, early], in_=o_words[:, early].bitcast(I32))
-        ends = [slice(S - CHUNK, S - CHUNK // 2), slice(S - CHUNK // 2, S)]
-        for cols in ends:
-            round_result(cols)
-        for cols in ends:
-            hand_on(cols)
+        hand_on(chunk(3), rounded[3])
 
         nc.scalar.dma_start(out=out_words[:, chunk(3)], in_=o_words[:, chunk(3)].bitcast(I32))
         for q in range(QUADRANTS):

@@ -65,7 +65,7 @@ def tile_picked_errfb_none_po_kernel(
         w2w = tile([P, N], I32, "w2w")
         w1s = tile([P, H], U8, "w1s")
         w2s = tile([P, N], U8, "w2s")
-        gn_t = placed([P, PACK], F32, "gn_t")
+        gn_t = tile([P, PACK], F32, "gn_t")
         ef_t = [tile([P, U], F32, f"ef{t}") for t in range(PACK)]
 
         nc.vector.memset(xs[:].bitcast(I32), 0)
@@ -79,7 +79,7 @@ def tile_picked_errfb_none_po_kernel(
         load_scale_rows(xs, 0, x_scales)
         nc.sync.dma_start(out=xw[:].bitcast(I32), in_=words(x_words))
         load_scale_rows(w1s, W1_ROW, w1_scales)
-        nc.sync.dma_start(out=gn_t[:], in_=gn.rearrange("(p t) o -> p (t o)", t=PACK))
+        nc.gpsimd.dma_start(out=gn_t[:], in_=gn.rearrange("(p t) o -> p (t o)", t=PACK))
         for t in range(PACK):
             nc.sync.dma_start(out=ef_t[t][:], in_=ef_rows[t])
         load_scale_rows(w2s, W2_ROW, w2_scales)
@@ -111,7 +111,7 @@ def tile_picked_errfb_none_po_kernel(
         xs_g = tile([P, S], U8, "xs_g")
         nc.vector.tensor_copy(xs_g[:], xs[:].indirect(offs_t[:]))
         w1sd = tile([P, H], U8, "w1sd")
-        xw_g = [tile([P, HALF], U32, "xw_g0"), placed([P, HALF], U32, "xw_g1")]
+        xw_g = [tile([P, HALF], U32, f"xw_g{h}") for h in range(2)]
         nc.vector.tensor_copy(xw_g[0][:], xw[:].indirect(entries(offs_t, halves[0])))
         deal_bytes(w1sd, w1s)
         nc.vector.tensor_copy(xw_g[1][:], xw[:].indirect(entries(offs_t, halves[1])))
@@ -146,10 +146,16 @@ def tile_picked_errfb_none_po_kernel(
                     stop=True,
                 )
 
+        on_vector = [(0, halves[0]), (1, halves[1])]
+        quarter_row = {}
+        for t, cols in on_vector:
+            quarter_row[t] = tile([P, HALF], F32, f"quarter_row{t}")
+            nc.scalar.copy(out=quarter_row[t][:], in_=quarter[:, t : t + 1].to_broadcast([P, HALF]))
+
         def look_up(t, cols):
             window = ef_t[t][:].indirect(entries(ent_t, cols))
-            if (t, cols) == (0, halves[1]):
-                nc.vector.tensor_copy(looked[t][:, cols], window)
+            if (t, cols) in on_vector:
+                nc.vector.tensor_tensor(scaled[t][:, cols], window, quarter_row[t][:], ALU.mult)
             else:
                 nc.scalar.activation(looked[t][:, cols], window, ACT.Copy)
 
@@ -173,9 +179,10 @@ def tile_picked_errfb_none_po_kernel(
 
         for t in range(PACK):
             for cols in halves:
-                look_up(t, cols)
-                if (t, cols) != (last_plane, halves[0]):
-                    scale(t, cols)
+                if (t, cols) not in on_vector:
+                    look_up(t, cols)
+                    if (t, cols) != (last_plane, halves[0]):
+                        scale(t, cols)
         w2d = tile([P, N], U32, "w2d")
         nc.scalar.copy(
             out=w2d[:].rearrange("p (u e r i) -> p r u i e", u=2, e=2, i=4),
@@ -183,11 +190,16 @@ def tile_picked_errfb_none_po_kernel(
         )
         whole = slice(0, S)
         w2sd = tile([P, N], U8, "w2sd")
-        for t in range(last_plane):
-            add(t, halves[0])
-            if t > 0:
-                clip(t - 1, whole)
-            add(t, halves[1])
+        look_up(0, halves[0])
+        add(0, halves[0])
+        add(0, halves[1])
+        look_up(1, halves[1])
+        clip(0, whole)
+        add(1, halves[1])
+        add(1, halves[0])
+        add(2, halves[0])
+        clip(1, whole)
+        add(2, halves[1])
         a_last = scaled[last_plane][:, halves[0]]
         nc.vector.tensor_tensor(a_last, y_part(last_plane, halves[0]), looked[last_plane][:, halves[0]], ALU.add)
         clip(2, whole)

@@ -181,8 +181,14 @@ def tile_picked_errfb_none_po_kernel(
             for cols in halves:
                 if (t, cols) not in on_vector:
                     look_up(t, cols)
-                    if (t, cols) != (last_plane, halves[0]):
+                    if t != last_plane:
                         scale(t, cols)
+        nc.scalar.activation(
+            scaled[last_plane][:, halves[1]],
+            looked[last_plane][:, halves[1]],
+            ACT.Copy,
+            scale=quarter[:, last_plane:PACK],
+        )
         w2d = tile([P, N], U32, "w2d")
         nc.scalar.copy(
             out=w2d[:].rearrange("p (u e r i) -> p r u i e", u=2, e=2, i=4),
@@ -211,10 +217,10 @@ def tile_picked_errfb_none_po_kernel(
 
         o_words = tile([P, S], U32, "o_words")
         o_scales = tile([P, S], U8, "o_scales")
-        res = tile([P, S // CHUNK, PACK, CHUNK], F32, "res")
-        rounded = {}
         out_rows = out_0.rearrange("(p t) j -> p t j", t=PACK)
         out_words = words(out_1)
+        pieces = [halves[0], slice(HALF, HALF + CHUNK), slice(HALF + CHUNK, S)]
+        res = [tile([P, PACK, cols.stop - cols.start], F32, f"res{c}") for c, cols in enumerate(pieces)]
 
         def woven_view(woven):
             return woven.rearrange("p (r i t) -> p r t i", t=PACK, i=2)
@@ -222,78 +228,77 @@ def tile_picked_errfb_none_po_kernel(
         def planes_view(planes):
             return planes.rearrange("p t (r i) -> p r t i", i=2)
 
-        def chunk(c):
-            return slice(CHUNK * c, CHUNK * (c + 1))
-
         def woven_columns(cols):
             return slice(PACK * cols.start, PACK * cols.stop)
 
-        def make_z(c):
-            z = placed([P, PACK * CHUNK], BF16, "z2", Z_AT) if c == 2 else tile([P, PACK * CHUNK], BF16, f"z{c}")
+        def make_z(c, z):
             nc.vector.scalar_tensor_tensor(
                 z[:].rearrange("p (i o) -> p o i", i=RUN),
-                cut[:, woven_columns(chunk(c))].rearrange("p (o i) -> p o i", i=RUN),
+                cut[:, woven_columns(pieces[c])].rearrange("p (o i) -> p o i", i=RUN),
                 3.0,
-                lin[:, woven_columns(chunk(c))].rearrange("p (o i) -> p o i", i=RUN),
+                lin[:, woven_columns(pieces[c])].rearrange("p (o i) -> p o i", i=RUN),
                 ALU.mult,
                 ALU.add,
             )
-            return z
 
-        def second_product(c, z, last=False):
-            zw = tile([P, CHUNK], U32, f"zw{c}")
-            zs = tile([P, CHUNK], U8, f"zs{c}")
+        def second_product(c, z, banks):
+            width = pieces[c].stop - pieces[c].start
+            zw = tile([P, width], U32, f"zw{c}")
+            zs = tile([P, width], U8, f"zs{c}")
             nc.vector.quantize_mx(out=zw[:].bitcast(FP8X4), scales=zs[:], in_=z[:])
-            bank = ps.tile([P, PACK, CHUNK], F32, name=f"o_ps{c}", tag=f"bank{(5 + c) % 8}")
-            for t in range(PACK):
-                nc.tensor.matmul_mx(
-                    out=bank[:, t, :],
-                    lhsT=w2d[:, P * t : P * (t + 1)].bitcast(FP8X4),
-                    lhsT_scale=w2sd[W2_ROW:P, P * t : P * (t + 1)],
-                    rhs=zw[:].bitcast(FP8X4),
-                    rhs_scale=zs[:],
-                    start=True,
-                    stop=True,
-                )
-            nc.scalar.copy(
-                out=res[:, c].rearrange("p t (r i) -> p t r i", i=RUN),
-                in_=bank[:].rearrange("p t (i r) -> p t r i", i=RUN),
-            )
-            if last:
+            per_bank = PACK // len(banks)
+            for b, number in enumerate(banks):
+                planes = slice(per_bank * b, per_bank * (b + 1))
+                bank = ps.tile([P, per_bank, width], F32, name=f"o_ps{c}{b}", tag=f"bank{number}")
+                for t in range(planes.start, planes.stop):
+                    nc.tensor.matmul_mx(
+                        out=bank[:, t - planes.start, :],
+                        lhsT=w2d[:, P * t : P * (t + 1)].bitcast(FP8X4),
+                        lhsT_scale=w2sd[W2_ROW:P, P * t : P * (t + 1)],
+                        rhs=zw[:].bitcast(FP8X4),
+                        rhs_scale=zs[:],
+                        start=True,
+                        stop=True,
+                    )
                 nc.scalar.copy(
-                    out=rounded[c].rearrange("p (r i t) -> p r i t", i=RUN, t=PACK),
-                    in_=bank[:].rearrange("p t (i r) -> p r i t", i=RUN),
+                    out=res[c][:, planes, :].rearrange("p t (r i) -> p t r i", i=RUN),
+                    in_=bank[:].rearrange("p t (i r) -> p t r i", i=RUN),
                 )
-            nc.sync.dma_start(out=out_rows[:, :, chunk(c)], in_=res[:, c])
+                nc.sync.dma_start(out=out_rows[:, planes, pieces[c]], in_=res[c][:, planes, :])
+            return bank
 
-        def round_result(c):
-            nc.vector.tensor_copy(out=woven_view(rounded[c]), in_=planes_view(res[:, c]))
+        def round_result(c, woven):
+            nc.vector.tensor_copy(out=woven_view(woven), in_=planes_view(res[c][:]))
 
         def hand_on(cols, woven):
             nc.vector.quantize_mx(out=o_words[:, cols].bitcast(FP8X4), scales=o_scales[:, cols], in_=woven)
 
-        rounded[3] = tile([P, PACK * CHUNK], BF16, "rounded3")[:]
-
-        z0 = make_z(0)
+        z0 = tile([P, PACK * HALF], BF16, "z0")
+        z1 = placed([P, PACK * CHUNK], BF16, "z1", Z_AT)
+        z2 = tile([P, PACK * CHUNK], BF16, "z2")
+        make_z(0, z0)
         add(3, halves[1])
-        second_product(0, z0)
-        z1 = make_z(1)
+        second_product(0, z0, [5, 6])
         clip(last_plane, halves[1])
-        second_product(1, z1)
-        z2 = make_z(2)
-        z3 = make_z(3)
-        second_product(2, z2)
-        second_product(3, z3, last=True)
-        first_three = placed([P, 3 * PACK * CHUNK], BF16, "rounded012", Z_AT)
-        for c in range(3):
-            rounded[c] = first_three[:, woven_columns(chunk(c))]
-            round_result(c)
-        early = slice(0, 3 * CHUNK)
-        hand_on(early, first_three[:])
+        make_z(1, z1)
+        make_z(2, z2)
+        second_product(1, z1, [7])
+        last_bank = second_product(2, z2, [0])
+        rounded_last = tile([P, PACK * CHUNK], BF16, "rounded_last")
+        nc.scalar.copy(
+            out=rounded_last[:].rearrange("p (r i t) -> p r i t", i=RUN, t=PACK),
+            in_=last_bank[:].rearrange("p t (i r) -> p r i t", i=RUN),
+        )
+        rounded = placed([P, 3 * PACK * CHUNK], BF16, "rounded", Z_AT)
+        for c in range(2):
+            round_result(c, rounded[:, woven_columns(pieces[c])])
+        for c in range(2):
+            hand_on(pieces[c], rounded[:, woven_columns(pieces[c])])
+        early = slice(0, pieces[2].start)
         nc.sync.dma_start(out=out_words[:, early], in_=o_words[:, early].bitcast(I32))
-        hand_on(chunk(3), rounded[3])
+        hand_on(pieces[2], rounded_last[:])
 
-        nc.scalar.dma_start(out=out_words[:, chunk(3)], in_=o_words[:, chunk(3)].bitcast(I32))
+        nc.scalar.dma_start(out=out_words[:, pieces[2]], in_=o_words[:, pieces[2]].bitcast(I32))
         for q in range(QUADRANTS):
             queue = nc.scalar if q % 2 else nc.sync
             queue.dma_start(

@@ -160,7 +160,11 @@ def tile_picked_errfb_none_po_kernel(
                 nc.scalar.activation(looked[t][:, cols], window, ACT.Copy)
 
         def scale(t, cols):
-            nc.gpsimd.tensor_scalar(scaled[t][:, cols], looked[t][:, cols], quarter[:, t : t + 1], 0.0, ALU.mult, ALU.add)
+            factor = quarter[:, t : t + 1]
+            if t in (1, 2):
+                nc.gpsimd.tensor_scalar(scaled[t][:, cols], looked[t][:, cols], factor, 0.0, ALU.mult, ALU.add)
+            else:
+                nc.scalar.activation(scaled[t][:, cols], looked[t][:, cols], ACT.Copy, scale=factor)
 
         def add(t, cols):
             nc.vector.scalar_tensor_tensor(
@@ -181,14 +185,8 @@ def tile_picked_errfb_none_po_kernel(
             for cols in halves:
                 if (t, cols) not in on_vector:
                     look_up(t, cols)
-                    if t != last_plane:
+                    if (t, cols) != (last_plane, halves[0]):
                         scale(t, cols)
-        nc.scalar.activation(
-            scaled[last_plane][:, halves[1]],
-            looked[last_plane][:, halves[1]],
-            ACT.Copy,
-            scale=quarter[:, last_plane:PACK],
-        )
         w2d = tile([P, N], U32, "w2d")
         nc.scalar.copy(
             out=w2d[:].rearrange("p (u e r i) -> p r u i e", u=2, e=2, i=4),

@@ -276,12 +276,12 @@ def tile_picked_errfb_none_po_kernel(
         z2 = tile([P, PACK * CHUNK], BF16, "z2")
         make_z(0, z0)
         add(3, halves[1])
-        second_product(0, z0, [5, 6])
+        second_product(0, z0, [5, 6, 7, 4])
         clip(last_plane, halves[1])
         make_z(1, z1)
         make_z(2, z2)
-        second_product(1, z1, [7])
-        last_bank = second_product(2, z2, [0])
+        second_product(1, z1, [0])
+        last_bank = second_product(2, z2, [1])
         rounded_last = tile([P, PACK * CHUNK], BF16, "rounded_last")
         nc.scalar.copy(
             out=rounded_last[:].rearrange("p (r i t) -> p r i t", i=RUN, t=PACK),

@@ -280,8 +280,8 @@ def tile_picked_errfb_none_po_kernel(
         clip(last_plane, halves[1])
         make_z(1, z1)
         make_z(2, z2)
-        second_product(1, z1, [0])
-        last_bank = second_product(2, z2, [1])
+        second_product(1, z1, [0, 1])
+        last_bank = second_product(2, z2, [2])
         rounded_last = tile([P, PACK * CHUNK], BF16, "rounded_last")
         nc.scalar.copy(
             out=rounded_last[:].rearrange("p (r i t) -> p r i t", i=RUN, t=PACK),
@@ -292,14 +292,12 @@ def tile_picked_errfb_none_po_kernel(
             round_result(c, rounded[:, woven_columns(pieces[c])])
         for c in range(2):
             hand_on(pieces[c], rounded[:, woven_columns(pieces[c])])
-        early = slice(0, pieces[2].start)
-        nc.sync.dma_start(out=out_words[:, early], in_=o_words[:, early].bitcast(I32))
         hand_on(pieces[2], rounded_last[:])
 
-        nc.scalar.dma_start(out=out_words[:, pieces[2]], in_=o_words[:, pieces[2]].bitcast(I32))
-        for q in range(QUADRANTS):
-            queue = nc.scalar if q % 2 else nc.sync
+        nc.sync.dma_start(out=out_words, in_=o_words[:].bitcast(I32))
+        for r in range(ROWS):
+            queue = nc.sync if r == 0 else nc.scalar
             queue.dma_start(
-                out=out_2[0, ROWS * q : ROWS * (q + 1), :].bitcast(I32),
-                in_=o_scales[QUADRANT * q : QUADRANT * q + ROWS, :].bitcast(I32),
+                out=out_2[0, r : ROWS * QUADRANTS : ROWS, :].bitcast(I32),
+                in_=o_scales[r:P:QUADRANT, :].bitcast(I32),
             )

@@ -74,12 +74,12 @@ def tile_picked_errfb_none_po_kernel(
 
         ef_rows = ef.rearrange("(p t) u -> t p u", t=PACK)
         nc.sync.dma_start(offs_t[:], offs)
-        nc.sync.dma_start(ent_t[:], ent)
+        nc.sync.dma_start(out=gn_t[:], in_=gn.rearrange("(p t) o -> p (t o)", t=PACK))
         nc.sync.dma_start(out=w1w[:], in_=words(w1_words))
         load_scale_rows(xs, 0, x_scales)
         nc.sync.dma_start(out=xw[:].bitcast(I32), in_=words(x_words))
         load_scale_rows(w1s, W1_ROW, w1_scales)
-        nc.gpsimd.dma_start(out=gn_t[:], in_=gn.rearrange("(p t) o -> p (t o)", t=PACK))
+        nc.sync.dma_start(ent_t[:], ent)
         for t in range(PACK):
             nc.sync.dma_start(out=ef_t[t][:], in_=ef_rows[t])
         load_scale_rows(w2s, W2_ROW, w2_scales)

@@ -73,9 +73,9 @@ def tile_picked_errfb_none_po_kernel(
         nc.vector.memset(w2s[:].bitcast(I32), 0)
 
         ef_rows = ef.rearrange("(p t) u -> t p u", t=PACK)
+        nc.sync.dma_start(out=w1w[:], in_=words(w1_words))
         nc.sync.dma_start(offs_t[:], offs)
         nc.sync.dma_start(out=gn_t[:], in_=gn.rearrange("(p t) o -> p (t o)", t=PACK))
-        nc.sync.dma_start(out=w1w[:], in_=words(w1_words))
         load_scale_rows(xs, 0, x_scales)
         nc.sync.dma_start(out=xw[:].bitcast(I32), in_=words(x_words))
         load_scale_rows(w1s, W1_ROW, w1_scales)

from contextlib import ExitStack

import concourse.mybir as mybir

K, T, S, N, H, U = 512, 2048, 512, 512, 512, 1024
FLOPS = 2 * K * H * S + 2 * H * N * S

F32 = mybir.dt.float32
BF16 = mybir.dt.bfloat16
I32 = mybir.dt.int32
U32 = mybir.dt.uint32
U16 = mybir.dt.uint16
U8 = mybir.dt.uint8
FP8X4 = mybir.dt.float8_e4m3fn_x4
ALU = mybir.AluOpType
ACT = mybir.ActivationFunctionType

P = 128
PACK = 4
QUADRANT = 32
GROUP = 16
QUADRANTS = P // QUADRANT
ROWS = 4
HALF = S // 2
CHUNK = S // 4
Z_AT = 4 * HALF
RUN = 4
W1_ROW = 4
W2_ROW = 8


def tile_picked_errfb_none_po_kernel(
    tc, x_words, x_scales, w1_words, w1_scales, ef, gn, w2_words, w2_scales, offs, ent, out_0, out_1, out_2
):
    nc = tc.nc
    with ExitStack() as ctx:
        sb = ctx.enter_context(tc.tile_pool(name="sb", bufs=1))
        shared = ctx.enter_context(tc.tile_pool(name="shared", bufs=1))
        ps = ctx.enter_context(tc.psum_pool(name="ps", bufs=1))

        def tile(shape, dtype, name):
            return sb.tile(shape, dtype, name=name, align_bytes=64)

        def placed(shape, dtype, name, offset=0):
            return shared.tile(shape, dtype, name=name, align_bytes=64, offset=offset)

        def words(dram):
            return dram[0].rearrange("p n t -> p (n t)").bitcast(I32)

        def load_scale_rows(scale_tile, first, dram):
            for r in range(ROWS):
                nc.sync.dma_start(
                    out=scale_tile[first + r : P : QUADRANT, :].bitcast(I32),
                    in_=dram[0, r : ROWS * QUADRANTS : ROWS, :].bitcast(I32),
                )

        halves = [slice(0, HALF), slice(HALF, S)]
        last_plane = PACK - 1

        offs_t = tile([P, S // GROUP], U16, "offs_t")
        ent_t = tile([P, S // GROUP], U16, "ent_t")
        xw = tile([P, T], U32, "xw")
        xs = tile([P, T], U8, "xs")
        w1w = tile([P, H], I32, "w1w")
        w2w = tile([P, N], I32, "w2w")
        w1s = tile([P, H], U8, "w1s")
        w2s = tile([P, N], U8, "w2s")
        gn_t = tile([P, PACK], F32, "gn_t")
        ef_t = [tile([P, U], F32, f"ef{t}") for t in range(PACK)]

        nc.vector.memset(xs[:].bitcast(I32), 0)
        nc.vector.memset(w1s[:].bitcast(I32), 0)
        nc.vector.memset(w2s[:].bitcast(I32), 0)

        ef_rows = ef.rearrange("(p t) u -> t p u", t=PACK)
        nc.sync.dma_start(out=w1w[:], in_=words(w1_words))
        nc.sync.dma_start(offs_t[:], offs)
        nc.sync.dma_start(out=gn_t[:], in_=gn.rearrange("(p t) o -> p (t o)", t=PACK))
        load_scale_rows(xs, 0, x_scales)
        nc.sync.dma_start(out=xw[:].bitcast(I32), in_=words(x_words))
        load_scale_rows(w1s, W1_ROW, w1_scales)
        nc.sync.dma_start(ent_t[:], ent)
        for t in range(PACK):
            nc.sync.dma_start(out=ef_t[t][:], in_=ef_rows[t])
        load_scale_rows(w2s, W2_ROW, w2_scales)
        nc.sync.dma_start(out=w2w[:], in_=words(w2_words))

        quarter = tile([P, PACK], F32, "quarter")
        high = tile([P, PACK], F32, "high")
        nc.scalar.activation(quarter[:], gn_t[:], ACT.Copy, scale=0.25)
        low = tile([P, PACK], F32, "low")
        nc.scalar.activation(high[:], gn_t[:], ACT.Abs, scale=0.125)
        nc.scalar.activation(low[:], high[:], ACT.Copy, scale=-1.0)

        def deal_words(dst, src):
            nc.vector.tensor_copy(
                out=dst[:].rearrange("p (u e r i) -> p r u i e", u=2, e=2, i=4),
                in_=src[:].rearrange("p (r i u e) -> p r u i e", u=2, e=2, i=4),
            )

        def deal_bytes(dst, src):
            nc.vector.tensor_copy(
                out=dst[:].rearrange("p (t m) -> p t m", t=PACK), in_=src[:].rearrange("p (m t) -> p t m", t=PACK)
            )

        def entries(list_tile, cols):
            return list_tile[:, cols.start // GROUP : cols.stop // GROUP]

        w1d = tile([P, H], I32, "w1d")
        deal_words(w1d, w1w)
        xs_g = tile([P, S], U8, "xs_g")
        nc.vector.tensor_copy(xs_g[:], xs[:].indirect(offs_t[:]))
        w1sd = tile([P, H], U8, "w1sd")
        xw_g = [tile([P, HALF], U32, f"xw_g{h}") for h in range(2)]
        nc.vector.tensor_copy(xw_g[0][:], xw[:].indirect(entries(offs_t, halves[0])))
        deal_bytes(w1sd, w1s)
        nc.vector.tensor_copy(xw_g[1][:], xw[:].indirect(entries(offs_t, halves[1])))

        looked = [tile([P, S], F32, f"looked{t}") for t in range(PACK)]
        scaled = [tile([P, S], F32, f"scaled{t}") for t in range(PACK)]
        lin = tile([P, PACK * S], F32, "lin")
        cut = tile([P, PACK * S], F32, "cut")

        def runs(plane):
            return plane.rearrange("p (r i) -> p r i", i=RUN)

        def plane_of(term, t, cols):
            view = term[:].rearrange("p (r t i) -> p t r i", t=PACK, i=RUN)
            return view[:, t, cols.start // RUN : cols.stop // RUN, :]

        y = [ps.tile([P, S], F32, name=f"y_ps{t}", tag=f"bank{t}") for t in range(PACK)]
        y_first = ps.tile([P, HALF], F32, name="y_first", tag="bank4")

        def y_part(t, cols):
            return y_first[:] if (t, cols) == (0, halves[0]) else y[t][:, cols]

        for t in range(PACK):
            for h, cols in enumerate(halves):
                nc.tensor.matmul_mx(
                    out=y_part(t, cols),
                    lhsT=w1d[:, P * t : P * (t + 1)].bitcast(FP8X4),
                    lhsT_scale=w1sd[W1_ROW:P, P * t : P * (t + 1)],
                    rhs=xw_g[h][:].bitcast(FP8X4),
                    rhs_scale=xs_g[:, cols],
                    start=True,
                    stop=True,
                )

        on_vector = [(0, halves[0]), (1, halves[1])]
        quarter_row = {}
        for t, cols in on_vector:
            quarter_row[t] = tile([P, HALF], F32, f"quarter_row{t}")
            nc.scalar.copy(out=quarter_row[t][:], in_=quarter[:, t : t + 1].to_broadcast([P, HALF]))

        def look_up(t, cols):
            window = ef_t[t][:].indirect(entries(ent_t, cols))
            if (t, cols) in on_vector:
                nc.vector.tensor_tensor(scaled[t][:, cols], window, quarter_row[t][:], ALU.mult)
            else:
                nc.scalar.activation(looked[t][:, cols], window, ACT.Copy)

        def scale(t, cols):
            factor = quarter[:, t : t + 1]
            if t in (1, 2):
                nc.gpsimd.tensor_scalar(scaled[t][:, cols], looked[t][:, cols], factor, 0.0, ALU.mult, ALU.add)
            else:
                nc.scalar.activation(scaled[t][:, cols], looked[t][:, cols], ACT.Copy, scale=factor)

        def add(t, cols):
            nc.vector.scalar_tensor_tensor(
                plane_of(lin, t, cols),
                runs(y_part(t, cols)),
                quarter[:, t : t + 1],
                runs(scaled[t][:, cols]),
                ALU.mult,
                ALU.add,
            )

        def clip(t, cols):
            nc.vector.tensor_scalar(
                plane_of(cut, t, cols), plane_of(lin, t, cols), high[:, t : t + 1], low[:, t : t + 1], ALU.min, ALU.max
            )

        for t in range(PACK):
            for cols in halves:
                if (t, cols) not in on_vector:
                    look_up(t, cols)
                    if (t, cols) != (last_plane, halves[0]):
                        scale(t, cols)
        w2d = tile([P, N], U32, "w2d")
        nc.scalar.copy(
            out=w2d[:].rearrange("p (u e r i) -> p r u i e", u=2, e=2, i=4),
            in_=w2w[:].bitcast(U32).rearrange("p (r i u e) -> p r u i e", u=2, e=2, i=4),
        )
        whole = slice(0, S)
        w2sd = tile([P, N], U8, "w2sd")
        look_up(0, halves[0])
        add(0, halves[0])
        add(0, halves[1])
        look_up(1, halves[1])
        clip(0, whole)
        add(1, halves[1])
        add(1, halves[0])
        add(2, halves[0])
        clip(1, whole)
        add(2, halves[1])
        a_last = scaled[last_plane][:, halves[0]]
        nc.vector.tensor_tensor(a_last, y_part(last_plane, halves[0]), looked[last_plane][:, halves[0]], ALU.add)
        clip(2, whole)
        nc.vector.tensor_scalar(
            plane_of(lin, last_plane, halves[0]), runs(a_last), quarter[:, last_plane:PACK], None, ALU.mult
        )
        deal_bytes(w2sd, w2s)
        clip(3, halves[0])

        o_words = tile([P, S], U32, "o_words")
        o_scales = tile([P, S], U8, "o_scales")
        out_rows = out_0.rearrange("(p t) j -> p t j", t=PACK)
        out_words = words(out_1)
        pieces = [halves[0], slice(HALF, HALF + CHUNK), slice(HALF + CHUNK, S)]
        res = [tile([P, PACK, cols.stop - cols.start], F32, f"res{c}") for c, cols in enumerate(pieces)]

        def woven_view(woven):
            return woven.rearrange("p (r i t) -> p r t i", t=PACK, i=2)

        def planes_view(planes):
            return planes.rearrange("p t (r i) -> p r t i", i=2)

        def woven_columns(cols):
            return slice(PACK * cols.start, PACK * cols.stop)

        def make_z(c, z):
            nc.vector.scalar_tensor_tensor(
                z[:].rearrange("p (i o) -> p o i", i=RUN),
                cut[:, woven_columns(pieces[c])].rearrange("p (o i) -> p o i", i=RUN),
                3.0,
                lin[:, woven_columns(pieces[c])].rearrange("p (o i) -> p o i", i=RUN),
                ALU.mult,
                ALU.add,
            )

        def second_product(c, z, banks):
            width = pieces[c].stop - pieces[c].start
            zw = tile([P, width], U32, f"zw{c}")
            zs = tile([P, width], U8, f"zs{c}")
            nc.vector.quantize_mx(out=zw[:].bitcast(FP8X4), scales=zs[:], in_=z[:])
            per_bank = PACK // len(banks)
            for b, number in enumerate(banks):
                planes = slice(per_bank * b, per_bank * (b + 1))
                bank = ps.tile([P, per_bank, width], F32, name=f"o_ps{c}{b}", tag=f"bank{number}")
                for t in range(planes.start, planes.stop):
                    nc.tensor.matmul_mx(
                        out=bank[:, t - planes.start, :],
                        lhsT=w2d[:, P * t : P * (t + 1)].bitcast(FP8X4),
                        lhsT_scale=w2sd[W2_ROW:P, P * t : P * (t + 1)],
                        rhs=zw[:].bitcast(FP8X4),
                        rhs_scale=zs[:],
                        start=True,
                        stop=True,
                    )
                nc.scalar.copy(
                    out=res[c][:, planes, :].rearrange("p t (r i) -> p t r i", i=RUN),
                    in_=bank[:].rearrange("p t (i r) -> p t r i", i=RUN),
                )
                nc.sync.dma_start(out=out_rows[:, planes, pieces[c]], in_=res[c][:, planes, :])
            return bank

        def round_result(c, woven):
            nc.vector.tensor_copy(out=woven_view(woven), in_=planes_view(res[c][:]))

        def hand_on(cols, woven):
            nc.vector.quantize_mx(out=o_words[:, cols].bitcast(FP8X4), scales=o_scales[:, cols], in_=woven)

        z0 = tile([P, PACK * HALF], BF16, "z0")
        z1 = placed([P, PACK * CHUNK], BF16, "z1", Z_AT)
        z2 = tile([P, PACK * CHUNK], BF16, "z2")
        make_z(0, z0)
        add(3, halves[1])
        second_product(0, z0, [5, 6, 7, 4])
        clip(last_plane, halves[1])
        make_z(1, z1)
        make_z(2, z2)
        second_product(1, z1, [0, 1])
        last_bank = second_product(2, z2, [2])
        rounded_last = tile([P, PACK * CHUNK], BF16, "rounded_last")
        nc.scalar.copy(
            out=rounded_last[:].rearrange("p (r i t) -> p r i t", i=RUN, t=PACK),
            in_=last_bank[:].rearrange("p t (i r) -> p r i t", i=RUN),
        )
        rounded = placed([P, 3 * PACK * CHUNK], BF16, "rounded", Z_AT)
        for c in range(2):
            round_result(c, rounded[:, woven_columns(pieces[c])])
        for c in range(2):
            hand_on(pieces[c], rounded[:, woven_columns(pieces[c])])
        hand_on(pieces[2], rounded_last[:])

        nc.sync.dma_start(out=out_words, in_=o_words[:].bitcast(I32))
        for r in range(ROWS):
            queue = nc.sync if r == 0 else nc.scalar
            queue.dma_start(
                out=out_2[0, r : ROWS * QUADRANTS : ROWS, :].bitcast(I32),
                in_=o_scales[r:P:QUADRANT, :].bitcast(I32),
            )
